import numpy as np, ml_dtypes
CORES = [13,21,141,149]
N = 4
BF = ml_dtypes.bfloat16
V, R, C, LA, HL, RO, HM = 1792, 64, 3, 192, 144, 4, 2048
Z = V - 1
def climb(fa, v, n):
    for _ in range(n): v = fa[v]
    return v
def mates(rng, fa, dp, a, e):
    key = np.arange(V)
    for _ in range(C): key = np.where(dp[key] > e, fa[key], key)
    o = np.argsort(key[:Z], kind="stable"); ks = key[o]; lo = np.searchsorted(ks, key[a]); hi = np.searchsorted(ks, key[a], side="right")
    return o[lo + (rng.random(a.shape) * (hi - lo)).astype(np.int64)]
def levels(c, top):
    m = V - 1 - R; t = int(np.sum(c)); n = [m * int(i) // t for i in c]; n[0] = min(n[0], top * R)
    for i in range(1, C): n[i] = min(n[i], 14 * n[i - 1])
    n[C - 1] += m - sum(n)
    return n
def forest(rng, n, sp, roots, num, forced):
    kd = np.full((16, V), Z); fa = np.arange(V); dp = np.zeros(V, np.int64); up = roots; pos = 0
    for d in range(C):
        key = rng.exponential(1.0, (len(up), 16)) * np.exp2(rng.integers(-sp, sp + 1, (len(up), 1)))
        for i, (u, j) in enumerate(forced[d] if d < len(forced) else ()): key[u, j] = i - 1000.0
        o = np.argsort(key, axis=None)[:n[d]]; nodes = num[pos:pos + n[d]]; pos += n[d]; u = up[o >> 4]
        kd[o & 15, u] = nodes; fa[nodes] = u; dp[nodes] = d + 1; up = nodes
    return kd, fa, dp
def lanes(rng, fa, dp):
    a = rng.integers(0, Z, LA); b = rng.integers(0, V, LA); p = rng.integers(0, C + 1, LA)
    for e in range(C): b = np.where(p == e, mates(rng, fa, dp, a, e), b)
    return a, b
def base(rng, plan=None):
    kd = np.zeros((N, 8, 16, V), np.int64); fa = np.zeros((N, 8, V), np.int64); dp = fa.copy(); pa = np.zeros((N, 8, LA), np.int64); pb = pa.copy()
    for q in range(N):
        for g in range(8):
            c, top, sp = plan(rng, q, g) if plan else (rng.integers(2, 5, C), 8, 3)
            kd[q, g], fa[q, g], dp[q, g] = forest(rng, levels(c, top), sp, rng.permutation(R), R + rng.permutation(V - 1 - R), ())
            pa[q, g], pb[q, g] = lanes(rng, fa[q, g], dp[q, g])
    x = (rng.random((N, 8, 16, V)) * 256 * np.exp2(rng.integers(-2, 1, (N, 8, 1, V)))).astype(np.int64)
    return dict(x=x, kd=kd, fa=fa, dp=dp, pa=pa, pb=pb, w=rng.integers(0, 256, (N, 8, 16, 1)))
def pack(s):
    x = s["x"].copy(); x[..., Z] = 0; i4 = lambda v, *sh: np.ascontiguousarray(v.reshape(sh)).astype(np.int32)
    return {"xs": np.ascontiguousarray(x.reshape(N, 128, V)).astype(np.float32).astype(BF), "kd": i4(s["kd"], N, 128, V), "fa": i4(s["fa"], N, 8, V), "dp": i4(s["dp"], N, 8, V),
            "pa": i4(s["pa"], N, 8, LA), "pb": i4(s["pb"], N, 8, LA), "wt": i4(s["w"], N, 128, 1)}
def setup_inputs(rng):
    return pack(base(rng))
def setup_inputs_spread(rng):
    s = base(rng, lambda r, q, g: (r.integers(2, 5, C), 8, 6))
    s["x"] = (rng.random((N, 8, 16, V)) * np.exp2(rng.integers(0, 9, (N, 8, 1, V)))).astype(np.int64)
    s["w"] = (rng.random((N, 8, 16, 1)) * np.exp2(rng.integers(0, 9, (N, 8, 16, 1)))).astype(np.int64)
    return pack(s)
def setup_inputs_ends(rng):
    n = [2 * R] + [(36 * V // 100 - 2 * R) // (C - 2)] * (C - 2); n.append(V - 1 - R - sum(n)); s = base(rng)
    forced = ([(0, 0), (0, 15), (1, 0)], [(0, 0), (0, 7), (0, 14), (0, 15), (1, 0), (1, 3), (1, 15)], [(i, j) for i in range(7) for j in (0, 15)])
    k = rng.random((N, 8, 1, V)); x = 255 * rng.integers(0, 2, (N, 8, 16, V)); x = np.where(k < 0.35, 255, np.where(k < 0.6, 0, x)); w = 255 * rng.integers(0, 2, (N, 8, 16, 1))
    for q in range(N):
        for g in range(8):
            num = R + rng.permutation(V - 1 - R)
            for at, v in ((0, V - 3), (1, R), (2, V - 2), (n[0] + 3, V - 4), (n[0], R + 1)):
                j = int(np.flatnonzero(num == v)[0]); num[j] = num[at]; num[at] = v
            kd, fa, dp = forest(rng, n, 3, np.concatenate([np.array([R - 1, 0]), 1 + rng.permutation(R - 2)]), num, forced)
            s["kd"][q, g], s["fa"][q, g], s["dp"][q, g] = kd, fa, dp
            mode = (7 - g + N - 1 - q) % 4; A, B = V - 3, R; y = x[q, g]; fam = []
            for v in (A, B):
                c = kd[:, v]; c = c[c != Z]; t = kd[:, c].reshape(-1); fam.append((c, t[t != Z]))
            y[:, A] = 0; y[:, B] = 0
            for c, t in fam: y[:, c] = 255; y[:, t] = 255
            y[(q + g) % 16, fam[0][0]] = 254
            best = num[n[0] + 1:n[0] + 4] if (q + g) % 2 == 0 else num[n[0] + 3:n[0] + 4]
            y[:, best] = 255
            if mode == 0: w[q, g] = 255
            if mode == 1: y[:, fam[1][0]] = 0; y[:, fam[1][1]] = 0
            if mode == 2: y[:, fam[0][0]] = 0; y[:, fam[0][1]] = 0
            if mode == 3:
                o = rng.permutation(16)[:9]; y[o[:, None], fam[1][0][None]] = 0; y[o[:, None], fam[1][1][None]] = 0
            a, b = lanes(rng, fa, dp); end = rng.random(LA) < 0.72
            a = np.where(end, rng.choice(np.array([0, V - 2]), LA), a); b = np.where(end, rng.choice(np.array([0, Z]), LA), b)
            a = np.where(climb(fa, a, C) == R - 1, 0, a); a[LA - 1] = A; b[LA - 1] = B
            s["pa"][q, g], s["pb"][q, g] = a, b
    s["x"], s["w"] = x, w
    return pack(s)
def setup_inputs_corners(rng):
    def plan(r, q, g):
        return ((r.integers(2, 5, C), 8, 20), ([1] * (C - 1) + [8], 8, 3), ([8] + [1] * (C - 1), 16, 3), (r.integers(2, 5, C), 8, 0))[(q + g) % 4]
    s = base(rng, plan); k = rng.random((N, 8, 1, V)); s["x"] = np.where(k < 0.15, 255, np.where(k < 0.3, 0, s["x"]))
    for q in range(N):
        for g in range(8):
            fa, dp = s["fa"][q, g], s["dp"][q, g]; a = np.where(rng.random(LA) < 0.4, rng.choice(np.array([0, R - 1, R, V - 2]), LA), s["pa"][q, g]); t = rng.integers(0, 5, LA)
            b = np.where(t == 0, rng.choice(np.array([0, R - 1, R, V - 2, Z]), LA), np.where(t == 1, a, np.where(t == 2, fa[a], np.where(t == 3, mates(rng, fa, dp, a, 0), mates(rng, fa, dp, a, C - 2)))))
            s["pa"][q, g], s["pb"][q, g] = a, b
            u = (q + 2 * g) % 5
            if u == 0: s["w"][q, g] = 0
            if u == 1: s["w"][q, g] = 255
    return pack(s)
def setup_inputs_ties(rng):
    s = base(rng)
    for q in range(N):
        for g in range(8):
            m = rng.choice(np.array([0, 0, 0, 8, 9, 16]), V); y = 100 + (rng.permutation(16)[:, None] < m[None]).astype(np.int64); t = rng.random(V)
            if (q + g) % 3: y = np.where(t < 0.12, 0, np.where(t < 0.2, 255, y))
            s["x"][q, g] = y
    return pack(s)
def pairs(rng, s, q, g):
    left = V - 1 - R - 5 * LA; more = left // (C - 2); n = [LA, 2 * LA, 2 * LA + more] + [more] * (C - 3); n[C - 1] += V - 1 - R - sum(n)
    rows = np.argsort(rng.random((LA, 16)), axis=1)[:, :2]; slot = rng.integers(0, 16, 2 * LA); num = R + rng.permutation(V - 1 - R)
    forced = ((), [(i >> 1, int(rows[i >> 1, i & 1])) for i in range(2 * LA)], [(i, int(slot[i])) for i in range(2 * LA)])
    kd, fa, dp = forest(rng, n, 3, rng.permutation(R), num, forced)
    s["kd"][q, g], s["fa"][q, g], s["dp"][q, g] = kd, fa, dp
    at = np.zeros(V, np.int64); at[num[LA:3 * LA]] = np.arange(2 * LA); m = np.flatnonzero(dp == 3); t = at[fa[m]]
    win = rng.integers(0, 2, LA); hi = np.argsort(rng.random((16, LA)), axis=0) < rng.integers(9, 17, LA)[None]
    y = rng.integers(0, 64, (16, V)); x = s["x"][q, g]; low = np.flatnonzero((dp == 2) | (dp > 3)); x[:, low] = y[:, low]
    x[:, m] = 64 + y[:, m] + 128 * (hi[:, t >> 1] == ((t & 1) == win[t >> 1])[None]).astype(np.int64)
    o = rng.permutation(LA); flip = rng.integers(0, 2, LA)
    return num[LA + 2 * o + flip], num[LA + 2 * o + 1 - flip]
def fold(rng, s, q, g):
    roots = np.concatenate([1 + rng.permutation(R - 1), np.array([0])]); num = R + rng.permutation(V - 1 - R); rows = np.argsort(rng.random((8, 16)), axis=1)[:, :2]
    forced = ([(i >> 1, int(rows[i >> 1, i & 1])) for i in range(16)], [(i, int(rows[i >> 1, i & 1])) for i in range(16)])
    kd, fa, dp = forest(rng, levels(rng.integers(2, 5, C), 8), 3, roots, num, forced)
    s["kd"][q, g], s["fa"][q, g], s["dp"][q, g] = kd, fa, dp
    top = climb(fa, np.arange(V), C); x = s["x"][q, g]; x[:2, np.flatnonzero(top == 0)] = 0; x[2:, 0] = 100
    ln = np.concatenate([np.array([HL, LA - 1]), HL + 1 + rng.permutation(LA - HL - 2)[:6]]); off = (0, 0, 0, 0, 0, 0, -1, 1)
    for i in range(8):
        u = int(roots[i]); goal = (V + off[i] - 977 * int(ln[i])) & (HM - 1); c = kd[:, u]; c = c[c != Z]; c1, c2 = int(num[2 * i]), int(num[2 * i + 1])
        x[:, np.flatnonzero((top == u) & (dp > 0))] = 0
        x[0, c] = goal & 15; x[1, c] = goal >> 4; x[2:, c1] = 100; x[2:6, c2] = 255
        for v, val in ((c1, 200), (c2, 50)):
            t = kd[:, v]; t = t[t != Z]; x[2:, t] = val
    a, b = lanes(rng, fa, dp); apart = np.isin(top[a], np.concatenate([roots[:8], np.array([0])]))
    a = np.where(apart, roots[8 + rng.integers(0, R - 9, LA)], a); a[ln] = roots[:8]; b[ln] = Z
    s["w"][q, g] = 0; s["w"][q, g, 0] = 1; s["w"][q, g, 1] = 16
    return a, b
def setup_inputs_crowd(rng):
    s = base(rng)
    for q in range(N):
        for g in range(8):
            kd, fa = s["kd"][q, g], s["fa"][q, g]; kind = (q + g) % 7; cand = rng.permutation(np.flatnonzero(np.add.reduce((kd != Z).astype(np.int64), axis=0) >= 2))
            if kind < 2:
                P = cand[rng.integers(0, 3, LA)] if kind == 0 else cand[np.arange(LA) % len(cand)]
                o = np.argsort(rng.random((16, LA)) + 2 * (kd[:, P] == Z), axis=0); a, b = kd[o[0], P], kd[o[1], P]
            elif kind == 2:
                a = rng.integers(0, R, LA); b = rng.integers(0, R + 1, LA); b = np.where(b == R, Z, b)
            elif kind == 3:
                a = rng.integers(0, Z, LA); t = rng.integers(0, 4, LA); b = np.where(t < 2, a, np.where(t == 2, climb(fa, a, 1), climb(fa, a, 2)))
            elif kind == 4:
                a, b = pairs(rng, s, q, g)
            elif kind == 5:
                P = rng.permutation(np.unique(fa[R:Z])); P = P[np.arange(LA) % len(P)]
                a = kd[np.argmin(rng.random((16, LA)) + 2 * (kd[:, P] == Z), axis=0), P]; b = a.copy()
            else:
                a, b = fold(rng, s, q, g)
            s["pa"][q, g], s["pb"][q, g] = a, b
    return pack(s)
def check_inputs(d):
    bad = []
    for k, lo, hi in (("xs", 0, 255), ("kd", R, Z), ("fa", 0, Z), ("dp", 0, C), ("pa", 0, Z - 1), ("pb", 0, Z), ("wt", 0, 255)):
        v = np.asarray(d[k]).astype(np.float64)
        if not (np.min(v) >= lo and np.max(v) <= hi): bad.append("range of " + k)
        elif np.any(v != np.floor(v)): bad.append("whole numbers of " + k)
    if bad: return bad
    M = N * 8; f = np.asarray(d["fa"]).astype(np.int64).reshape(M, V); e = np.asarray(d["dp"]).astype(np.int64).reshape(M, V); k = np.asarray(d["kd"]).astype(np.int64).reshape(M, 16 * V)
    if np.any(np.asarray(d["xs"]).astype(np.float32)[..., Z] != 0): bad.append("last column of xs")
    own = np.concatenate([np.arange(R), np.array([Z])])
    if np.any(f[:, own] != own) or np.any(e[:, own] != 0): bad.append("roots")
    if np.any(f[:, R:Z] == Z) or np.any(e[:, R:Z] != np.take_along_axis(e, f[:, R:Z], 1) + 1): bad.append("fathers and depths")
    s = np.sort(k, axis=1)
    if np.any(s[:, :Z - R] != np.arange(R, Z)) or np.any(s[:, Z - R:] != Z): bad.append("every node a kid once")
    if np.any((k != Z) & (np.take_along_axis(f, k, 1) != np.tile(np.arange(V), 16))): bad.append("kids and fathers")
    return bad
def pick(t, ix):
    return np.take_along_axis(t, ix, 1)
def cols(t, ix):
    return np.take_along_axis(t, ix[:, None, :], 2)
def ring(x, k, p, o):
    m = k.shape[0]; K = cols(k, p)
    y = cols(x, K.reshape(m, 16 * LA)).reshape(m, 16, 16, LA)
    score = np.add.reduce(np.maximum(y - cols(x, o)[:, :, None, :], 0), axis=1)
    row = np.argmax(score, axis=1)
    lead = np.take_along_axis(K, row[:, None, :], 1)[:, 0]
    z = cols(x, cols(k, lead).reshape(m, 16 * LA)).reshape(m, 16, 16, LA)
    return K, row, lead, np.max(y, axis=2) + np.max(z, axis=2)
def reference(xs, kd, fa, dp, pa, pb, wt):
    M = N * 8; x = xs.astype(np.float32).astype(np.int32).reshape(M, 16, V); k = kd.astype(np.int64).reshape(M, 16, V); f = fa.astype(np.int64).reshape(M, V); e = dp.astype(np.int64).reshape(M, V)
    a = pa.astype(np.int64).reshape(M, LA); b = pb.astype(np.int64).reshape(M, LA); w = wt.astype(np.int64).reshape(M, 16, 1)
    lane = np.arange(LA); lower = np.tri(LA, k=-1, dtype=bool); at = np.arange(M)[:, None]
    asked = ((at // 8 + 1 + lane[None] % (N - 1)) % N) * 8 + at % 8
    for rnd in range(RO):
        for step in range(C):
            da, db, ga, gb = pick(e, a), pick(e, b), pick(f, a), pick(f, b)
            go = (da != db) | (ga != gb)
            a, b = np.where(go & (da >= db), ga, a), np.where(go & (db >= da), gb, b)
        F = pick(f, a); met = (a != b) & (F == pick(f, b))
        KA, rA, lA, UA = ring(x, k, a, b)
        KB, rB, lB, UB = ring(x, k, b, a)
        awin = met & (np.add.reduce((UA > UB).astype(np.int64), axis=1) >= 9)
        bwin = met & (np.add.reduce((UB > UA).astype(np.int64), axis=1) >= 9)
        first = ~np.any((F[:, :, None] == F[:, None, :]) & lower[None], axis=2)
        W, L = np.where(bwin, b, a), np.where(bwin, a, b); lW, lL = np.where(bwin, lB, lA), np.where(bwin, lA, lB); rW, rL = np.where(bwin, rB, rA), np.where(bwin, rA, rB)
        x2, k2, f2 = x.copy(), k.copy(), f.copy()
        m, i = np.nonzero(first & (awin | bwin))
        x2[m, :, W[m, i]] = (x[m, :, W[m, i]] + x[m, :, lW[m, i]]) >> 1
        m, i = np.nonzero(first & (awin | bwin) & (lW != Z) & (lL != Z))
        k2[m, rW[m, i], W[m, i]] = lL[m, i]; k2[m, rL[m, i], L[m, i]] = lW[m, i]
        f2[m, lW[m, i]] = L[m, i]; f2[m, lL[m, i]] = W[m, i]
        h = np.add.reduce(w * UA, axis=1) & (R - 1)
        m, i = np.nonzero(first & ~met)
        x2[m, :, a[m, i]] = (UA[m, :, i] + 2 * x[asked[m, i], :, h[m, i]]) >> 2
        kid = np.where(bwin[:, None, :], KB, KA)[:, lane & 15, lane]
        new = (np.add.reduce(w * (UA + UB), axis=1) + 977 * lane) & (HM - 1); new = np.where(new >= V, new - V, new)
        a = np.where(lW == Z, W, lW); b = np.where(lane < HL, kid, new)
        x, k, f = x2, k2, f2
    return {"yx": x.reshape(N, 128, V).astype(np.float32).astype(BF), "yf": f.reshape(N, 8, V).astype(np.float32)}

@@ -1,0 +1,510 @@
+from concourse.bass import DstId, RemoteDMATransfer
+from concourse.mybir import AluOpType as OP, ActivationFunctionType as AF
+
+V, R, LA, RO, Z = 1792, 64, 192, 4, 1791
+UO, DO, RT = 1792, 1984, 2176
+XC = RT + 192 * RO
+f, b, i4, u2 = "float32", "bfloat16", "int32", "uint16"
+
+
+def S_(shape, d):
+    return ("sbuf", shape, d)
+
+
+SCRATCH = {
+    "XW": S_([128, XC], f), "KDW": S_([128, 2176], i4), "FAW": S_([128, 2176], f),
+    "FAD": ("dram", [8, V], f), "FAI": S_([128, 112], i4), "DPI": S_([128, 112], i4), "DPF": S_([128, 112], f),
+    "FAC": S_([128, 112], f), "YFA": S_([128, 112], f), "YFB": S_([128, 112], f),
+    "PAI": S_([128, 384], i4), "PAF": S_([128, 384], f), "WTI": S_([128, 1], i4), "WTF": S_([128, 1], f),
+    "ONE": S_([128, 128], f), "IDF": S_([128, 128], f), "NIF": S_([128, 128], f),
+    "IDB": S_([128, 128], b), "NIB": S_([128, 128], b), "IHB": S_([128, 128], b),
+    "PR0": S_([128, 128], f), "PR1": S_([128, 128], f),
+    "P00": S_([128, 128], f), "P11": S_([128, 128], f), "P01": S_([128, 128], f), "P10": S_([128, 128], f),
+    "MGT": S_([128, 128], f), "MG": S_([128, 128], f), "B8T": S_([128, 128], f), "B8": S_([128, 128], f),
+    "D64": S_([128, 64], f), "D32": S_([128, 32], f), "MW": S_([128, 384], f),
+    "LS": S_([128, 2048], b), "LW": S_([128, 2048], b), "CJ": S_([128, 192], b),
+    "RST": S_([128, 384], f), "RSB": S_([128, 3072], b), "EQ": S_([128, 12, 208], b),
+    "EQS": S_([128, 12, 208], b), "TRI": S_([128, 12, 16], b), "TIN": S_([128, 192], f),
+    "PMI": S_([128, 1], i4), "PMJ": S_([128, 1], i4), "PMF": S_([128, 1], f), "L16": S_([128, 12], f), "LN": S_([128, 12], f),
+    "KTI": S_([128, 12], i4), "KTF": S_([128, 12], f), "KT3": S_([128, 12], f), "E1C": S_([128, 12], f),
+    "XD": S_([128, 12], f), "D4": S_([128, 48], f), "SL": S_([128, 3], f), "IOT": S_([128, V], f),
+    "CC": S_([128, 96], i4), "U0": S_([128, 24], u2), "U1": S_([128, 24], u2), "U2": S_([128, 24], u2),
+    "G": S_([128, 384], f), "SB": S_([128, 1152], f), "Y": S_([128, 5, 36], f),
+    "E0": S_([128, 3, 24], f), "E1": S_([128, 3, 24], f), "E2": S_([128, 3, 24], f), "H": S_([128, 72], f),
+    "DL": S_([128, 72], f), "PRD": S_([128, 72], f), "T1": S_([128, 24], f), "T2": S_([128, 24], f),
+    "PF": S_([128, 24], f), "F1": S_([128, 12], f), "FW": S_([128, 12], f),
+    "QQ": S_([128, 4, 2, 12], f), "QD": S_([128, 4, 12], f), "QP": S_([128, 4, 12], f), "Q": S_([128, 48], f),
+    "UAB": S_([128, 24], u2), "NE": S_([128, 12], f), "ME2": S_([128, 24], f), "UN": S_([128, 12], f), "THR": S_([128, 24], f),
+    "KL": S_([128, 384], u2), "KF": S_([128, 12, 2, 16], f), "KT": S_([128, 12, 32], f), "SD": S_([128, 384], f),
+    "XAB": S_([128, 384], b), "FR": S_([128, 192], u2), "CM": S_([128, 12], f), "CU": S_([128, 12], f), "CN": S_([128, 12], f),
+    "XA": S_([128, 3072], b), "XB": S_([128, 3072], b), "MA": S_([128, 192, 16], b), "MB": S_([128, 192, 16], b),
+    "YA": S_([128, 3072], b), "YB": S_([128, 3072], b),
+    "GA1": S_([128, 3072], b), "GB1": S_([128, 3072], b), "GA2": S_([128, 3072], b), "GB2": S_([128, 3072], b),
+    "RUN": S_([128, 192], f), "TT": S_([128, 192], f), "DD": S_([128, 192], f), "LSC": S_([128, 192], f),
+    "UL3": S_([128, 36], u2), "K2": S_([128, 384], u2), "ZF": S_([128, 24], f), "ZD": S_([128, 24], f), "ZP": S_([128, 24], f),
+    "NZ": S_([128, 12], f), "NZ2": S_([128, 12], f), "LR": S_([128, 384], f), "OH": S_([128, 384], f), "MM": S_([128, 384], f),
+    "NK": S_([128, 384], i4), "FV": S_([128, 384], f), "CMP": S_([128, 384], b), "WIN": S_([128, 24], f), "WON": S_([128, 12], f),
+    "SW": S_([128, 12], f), "E4": S_([128, 48], f), "EP": S_([128, 4, 12], f), "DS": S_([128, 48], f), "DU": S_([128, 48], u2),
+    "HI": S_([128, 12], i4), "HJ": S_([128, 12], i4), "BS": S_([128, 24], f), "B2": S_([128, 24], f), "B3": S_([128, 24], f),
+    "EU": S_([128, 24], u2), "OK1": S_([128, 12], f), "OK2": S_([128, 12], f), "DX": S_([128, 12], f), "DX2": S_([128, 12], f),
+    "XU": S_([128, 12], u2), "XE": S_([128, 192], f), "XS": S_([128, 192], f), "XN": S_([128, 192], i4),
+    "SI": S_([128, 3], i4), "SJ": S_([128, 3], i4), "SF": S_([128, 3], f),
+    "RB": S_([128, 64 * RO], f),
+}
+for _n in ("PXP", "PMX", "PKA", "PKB", "PD", "PC", "PH", "PS"):
+    SCRATCH[_n] = ("psum", [128, 512], f)
+SMALL, _w = {}, 0
+for _n in ("PMF L16 LN KTF KT3 E1C XD SL T1 T2 PF F1 FW NE ME2 UN THR CM CU CN ZF ZD ZP NZ NZ2 WIN WON SW BS B2 B3 "
+           "OK1 OK2 DX DX2 SF WTF").split():
+    SMALL[_n] = (_w, SCRATCH[_n][1][1])
+    _w += (SCRATCH[_n][1][1] + 3) // 4 * 4
+    del SCRATCH[_n]
+SCRATCH["SM"] = S_([128, _w], f)
+SCRATCH["PMX"] = ("psum", [128, 12, 32], f)
+SEMAPHORES = ["v", "a", "p", "gq"] + ["arr%d" % t for t in range(RO)] + ["ls%d" % t for t in range(RO)] + \
+    ["rl%d" % t for t in range(RO)] + ["rs"] + ["d%d" % k for k in range(20)] + ["g%d" % k for k in range(6)]
+
+
+def relay_of(core, dst, topo):
+    c = [x for x in topo.cores_of(core) if x != core and topo.may_write(x, dst)]
+    return sorted(c, key=lambda x: (topo.die(x) != topo.die(core), x))[0]
+
+
+def split(core, topo, T):
+    near = [d for d in T.cores if d != core and topo.may_write(core, d)]
+    far = [d for d in T.cores if d != core and not topo.may_write(core, d)]
+    return near, far, (relay_of(core, far[0], topo) if far else None)
+
+
+def land(T, src, dst, t):
+    k = (T.rank_of(src) - T.rank_of(dst) - 1) % len(T.cores)
+    return RT + 192 * t + 64 * k
+
+
+def did(d, src, topo):
+    rid, pid = topo.addr(d, src)
+    return DstId(rid=rid, pnc=pid)
+
+
+def bits(es):
+    return sum(1 << e for e in es)
+
+
+def relay_program(g, core, T, topo, src):
+    far = split(src, topo, T)[1]
+    es = [topo.engines(core, d) for d in far]
+    n = 0
+    for t in range(RO):
+        g.wait_ge(T.sem["rl%d" % t], 4)
+        tr = []
+        for k, d in enumerate(far):
+            c = land(T, src, d, t)
+            tr.append(RemoteDMATransfer(dst_ids=[did(d, core, topo)], dma_engine_mask=bits(es[k][4 * k:4 * k + 4]),
+                                        remote_sem=T.sem["arr%d" % t], srcs=[T.RB[:, 64 * t:64 * t + 64]], dsts=[T.XW[:, c:c + 64]]))
+            n += 4
+        g.remote_dma_fused(tr, local_sem=T.sem.rs)
+    g.wait_ge(T.sem.rs, n)
+
+
+def rank_program(g, core, T, topo):
+    if T.rank_of(core) is None:
+        for src in T.cores:
+            if split(src, topo, T)[2] == core:
+                relay_program(g, core, T, topo, src)
+        return
+    eng = {"v": g.vector, "a": g.scalar, "p": g.tensor, "gq": g, "s": g.sync}
+    acc, total, waited, snap = {}, {}, {}, {}
+    know = {q: {} for q in eng}
+
+    def do(q, call, W, Rd, sem=None, inc=1):
+        dma = sem is not None
+        me = "dma" if dma else q
+        need = {}
+
+        def want(e):
+            need[e[3]] = max(need.get(e[3], 0), e[4])
+        for n, lo, hi in Rd:
+            for e in acc.get(n, []):
+                if (e[0] < hi and lo < e[1] and e[2]) or (n in PS and e[5] != me):
+                    want(e)
+        for n, lo, hi in W:
+            for e in acc.get(n, []):
+                if (n in PS and e[5] != me) or (e[0] < hi and lo < e[1] and not (me == "p" and e[5] == "p")):
+                    want(e)
+        for s, val in need.items():
+            val = total.get(s, val) if s[0] in "d" or (s[0] == "g" and s != "gq") else val
+            if know[q].get(s, 0) < val:
+                eng[q].wait_ge(T.sem[s], val)
+                waited[s] = max(waited.get(s, 0), val)
+                for k, x in snap.get((s, val), {}).items():
+                    know[q][k] = max(know[q].get(k, 0), x)
+                know[q][s] = val
+        r = call()
+        s = sem if dma else q
+        r.then_inc(T.sem[s], inc)
+        total[s] = total.get(s, 0) + inc
+        snap[(s, total[s])] = dict(know[q])
+        for n, lo, hi in W:
+            acc[n] = [e for e in acc.get(n, []) if not (lo <= e[0] and e[1] <= hi)]
+            acc[n].append((lo, hi, True, s, total[s], me))
+        for n, lo, hi in Rd:
+            acc[n] = [e for e in acc.get(n, []) if not (not e[2] and e[0] == lo and e[1] == hi and e[5] == me and me != "dma")]
+            acc[n].append((lo, hi, False, s, total[s], me))
+
+    PS = ("PXP", "PMX", "PKA", "PKB", "PD", "PC", "PH", "PS")
+
+    def o(n, lo=0, hi=None, st=1):
+        if n in SMALL:
+            w0, w = SMALL[n]
+            n, lo, hi = "SM", w0 + lo, w0 + (w if hi is None else hi)
+        hi = T[n].shape[1] if hi is None else hi
+        return (T[n][:, lo:hi] if st == 1 else T[n][:, lo:hi:st]), [(n, lo, hi)]
+
+    def ind(n, lo, hi, on, oc, od):
+        return T[n][:, lo:hi].indirect(T[on][:, oc:od]), [(n, lo, hi), (on, oc, od)]
+
+    def scat(n, lo, hi, on, oc, od):
+        return T[n][:, lo:hi].indirect(T[on][:, oc:od]), [(n, lo, hi)], [(on, oc, od)]
+
+    def cp(out, in_):
+        do("v", lambda: g.vector.tensor_copy(out[0], in_[0]), out[1], in_[1] + (out[2] if len(out) > 2 else []))
+
+    def tt(out, x, y, op):
+        do("v", lambda: g.vector.tensor_tensor(out[0], x[0], y[0], op), out[1], x[1] + y[1])
+
+    def ts(out, x, s1, op0, s2=None, op1=None):
+        rd = list(x[1])
+        if not isinstance(s1, (int, float)):
+            rd += s1[1]
+            s1 = s1[0]
+        if op1 is None:
+            do("v", lambda: g.vector.tensor_scalar(out[0], x[0], s1, None, op0), out[1], rd)
+        else:
+            do("v", lambda: g.vector.tensor_scalar(out[0], x[0], s1, s2, op0, op1), out[1], rd)
+
+    def scan(out, d0, d1, op0, op1):
+        do("v", lambda: g.vector.tensor_tensor_scan(out[0], d0[0], d1[0], 0.0, op0, op1), out[1], d0[1] + d1[1])
+
+    def ms(x, c):
+        do("v", lambda: g.vector.memset(x[0], c), x[1], [])
+
+    def act(out, in_):
+        do("a", lambda: g.scalar.activation(out[0], in_[0], AF.Copy), out[1], in_[1])
+
+    def mm(out, l, r, st, sp):
+        do("p", lambda: g.tensor.matmul(out[0], l[0], r[0], st, sp), out[1], l[1] + r[1])
+
+    def iota(x, pat, base, cm):
+        do("gq", lambda: g.iota(x[0], pat, base, cm, allow_small_or_imprecise_dtypes=True), x[1], [])
+
+    def asel(out, x, pat, op, base, cm):
+        do("gq", lambda: g.affine_select(out[0], x[0], pat, op, 0.0, base, cm), out[1], x[1])
+
+    nd = [0, 0]
+
+    def dma(q, out, in_, W, Rd, sem=None):
+        if sem is None:
+            sem = ("g%d" % nd[1]) if q == "gq" else ("d%d" % nd[0])
+            nd[1 if q == "gq" else 0] += 1
+        do(q, lambda: eng[q].dma_start(out, in_), W, Rd, sem, 16)
+        return sem
+
+    for t in range(RO):
+        acc.setdefault("XW", []).append((RT + 192 * t, RT + 192 * t + 192, True, "arr%d" % t, 12, "dma"))
+        total["arr%d" % t] = 12
+
+    near, far, rel = split(core, topo, T)
+    en = topo.engines(core, near[0])[:4]
+    er = [e for e in topo.engines(core, rel) if e not in en][:4]
+
+    def send(t):
+        need = {}
+        for e in acc["XW"]:
+            if e[2] and e[0] < 64:
+                need[e[3]] = max(need.get(e[3], 0), e[4])
+        for s, val in need.items():
+            if know["gq"].get(s, 0) < val:
+                g.wait_ge(T.sem[s], val)
+                waited[s] = max(waited.get(s, 0), val)
+                know["gq"][s] = val
+        c = land(T, core, near[0], t)
+        g.remote_dma_fused([
+            RemoteDMATransfer(dst_ids=[did(near[0], core, topo)], dma_engine_mask=bits(en), remote_sem=T.sem["arr%d" % t],
+                              srcs=[T.XW[:, 0:64]], dsts=[T.XW[:, c:c + 64]]),
+            RemoteDMATransfer(dst_ids=[did(rel, core, topo)], dma_engine_mask=bits(er), remote_sem=T.sem["rl%d" % t],
+                              srcs=[T.XW[:, 0:64]], dsts=[T.RB[:, 64 * t:64 * t + 64]])], local_sem=T.sem["ls%d" % t])
+        total["ls%d" % t] = 8
+        acc["XW"].append((0, 64, False, "ls%d" % t, 8, "dma"))
+
+    dma("s", T.FAI[:], T.fa[:], [("FAI", 0, 112)], [])
+    dma("a", T.DPI[:], T.dp[:], [("DPI", 0, 112)], [])
+    dma("s", T.PAI[0:8, 0:192], T.pa[:], [("PAI", 0, 192)], [])
+    dma("s", T.PAI[0:8, 192:384], T.pb[:], [("PAI", 192, 384)], [])
+    dma("a", T.WTI[:], T.wt[:], [("WTI", 0, 1)], [])
+    dma("gq", T.XW[:, 0:V], T.xs[:], [("XW", 0, V)], [])
+    dma("s", T.KDW[:, 0:V], T.kd[:], [("KDW", 0, V)], [])
+
+    ms(o("ONE"), 1.0)
+    asel(o("MGT"), o("ONE"), [[1, 128]], OP.is_ge, 0, -16)
+    asel(o("B8"), o("MGT"), [[-1, 128]], OP.is_ge, 15, 16)
+    asel(o("IDF"), o("ONE"), [[-1, 128]], OP.is_equal, 0, 1)
+    ts(o("DPF"), o("DPI"), 0.125, OP.mult)
+    tt(o("FAC"), o("FAI"), o("DPF"), OP.add)
+    dma("s", T.FAD[:], T.FAC[:], [("FAD", 0, V)], [("FAC", 0, 112)])
+    for k in range(16):
+        q = "s" if k % 2 == 0 else "a"
+        dma(q, T.FAW[k:128:16, 0:V], T.FAD[:], [("FAW%d" % k, 0, V)], [("FAD", 0, V)], sem="d18" if q == "s" else "d19")
+    acc["FAW"] = [(0, V, True, "d18", 128, "dma"), (0, V, True, "d19", 128, "dma")]
+    send(0)
+    ms(o("PR0"), 0.0)
+    ms(o("PR1"), 0.0)
+    for k in range(4):
+        ms(o("PR0", 32 * k, 32 * k + 16), 2.0 ** -12)
+        ms(o("PR1", 32 * k + 16, 32 * k + 32), 2.0 ** -12)
+    asel(o("MGT"), o("ONE"), [[-16, 8], [0, 16]], OP.is_ge, 0, 1)
+    asel(o("MG"), o("MGT"), [[16, 8], [0, 16]], OP.is_ge, 15, -1)
+    iota(o("PMI"), [[1, 1]], 0, 1)
+    iota(o("L16"), [[16, 12]], 0, 0)
+    iota(o("TIN"), [[0, 12], [1, 16]], 0, 0)
+    iota(o("CJ"), [[0, 12], [-1, 16]], 15, 0)
+    asel(o("P00"), o("PR0"), [[-1, 128]], OP.is_equal, 0, 1)
+    asel(o("P11"), o("PR1"), [[-1, 128]], OP.is_equal, 0, 1)
+    asel(o("P01"), o("PR1"), [[-1, 128]], OP.is_equal, 16, 1)
+    asel(o("P10"), o("PR0"), [[-1, 128]], OP.is_equal, -16, 1)
+    iota(o("IOT"), [[1, V]], 0, 0)
+    tt(o("D64"), o("IDF", 0, 64), o("IDF", 64, 128), OP.add)
+    tt(o("D32"), o("D64", 0, 32), o("D64", 32, 64), OP.add)
+    tt(o("MW", 0, 16), o("D32", 0, 16), o("D32", 16, 32), OP.add)
+    for a0, n in ((16, 16), (32, 32), (64, 64), (128, 128), (256, 128)):
+        cp(o("MW", a0, a0 + n), o("MW", 0, n))
+    ms(o("RST"), 1.0)
+    ms(o("RST", 0, 384, 16), 0.0)
+    do("v", lambda: g.vector.tensor_copy(T.PAF[0:8, :], T.PAI[0:8, :]), [("PAF", 0, 384)], [("PAI", 0, 384)])
+    do("p", lambda: g.tensor.matmul(T.PC[:, 0:384], T.B8[0:8, :], T.PAF[0:8, :], True, True), [("PC", 0, 384)], [("B8", 0, 128), ("PAF", 0, 384)])
+    tt(o("G"), o("PC", 0, 384), o("MW"), OP.mult)
+    scan(o("SD"), o("RST"), o("G"), OP.mult, OP.add)
+    cp(o("U0"), o("SD", 15, 384, 16))
+    cp(o("CC", 0, 24), o("SD", 15, 384, 16))
+    ts(o("PMJ"), o("PMI"), 15, OP.bitwise_and)
+    cp(o("PMF"), o("PMJ"))
+    ts(o("LN"), o("L16"), o("PMF"), OP.add)
+    ts(o("KTI"), o("LN"), 1.0 / 3, OP.mult, -1.0 / 3, OP.add)
+    ts(o("KTF"), o("KTI"), -3.0, OP.mult)
+    tt(o("KT3"), o("LN"), o("KTF"), OP.add)
+    ts(o("E1C"), o("KT3"), 64.0, OP.mult, float(RT), OP.add)
+    ts(o("XD"), o("LN"), float(DO), OP.add)
+    for k in range(4):
+        ts(o("D4", 12 * k, 12 * k + 12), o("LN"), float(V + 192 * (k % 2)), OP.add)
+    ts(o("BS", 12, 24), o("LN"), float(UO), OP.add)
+    ts(o("SL"), o("LN", 9, 12), 977.0, OP.mult)
+    ms(o("RSB"), 1.0)
+    ms(o("RSB", 0, 3072, 16), 0.0)
+    do("v", lambda: g.vector.tensor_scalar(T.TRI[:], T.TIN[:], o("PMF")[0], None, OP.is_lt), [("TRI", 0, 12)], [("TIN", 0, 192)] + o("PMF")[1])
+    ms(o("LS"), 0.0)
+    for s in range(16):
+        ts(o("LS", 128 * s + s, 128 * s + 128, 16), o("MG", 0, 128, 16), 16.0, OP.mult)
+    ts(o("WTF"), o("WTI"), 1.0 / 16, OP.mult)
+    ts(o("LW"), o("LS"), o("WTF"), OP.mult)
+    cp(o("IDB"), o("IDF"))
+    ts(o("NIB"), o("IDF"), -1.0, OP.mult)
+    ts(o("IHB"), o("IDF"), 0.5, OP.mult)
+    ts(o("NIF"), o("IDF"), -1.0, OP.mult)
+    ms(o("XW", V, RT), 0.0)
+
+    def r3(n, ap, lo, hi):
+        return ap, [(n, lo, hi)]
+
+    def qq(k, side=None):
+        if side is None:
+            return T.QQ[:, k, :, :], [("QQ", 24 * k, 24 * k + 24)]
+        return T.QQ[:, k, side, :], [("QQ", 24 * k + 12 * side, 24 * k + 12 * side + 12)]
+
+    for rnd in range(RO):
+        last = rnd == RO - 1
+        for k in range(3):
+            tt(o("G"), ind("FAW", 0, V, "U%d" % k, 0, 24), o("MW"), OP.mult)
+            scan(o("SB", 384 * k, 384 * k + 384), o("RST"), o("G"), OP.mult, OP.add)
+            y = o("SB", 384 * k + 15, 384 * k + 384, 16)
+            ya = o("SB", 384 * k + 15, 384 * k + 192, 16)
+            if k < 2:
+                cp(o("U%d" % (k + 1)), y)
+            for row in ((k, k + 3) if k < 2 else (k,)):
+                act(r3("Y", T.Y[:, row, 0:24], 36 * row, 36 * row + 24), y)
+                act(r3("Y", T.Y[:, row, 24:36], 36 * row + 24, 36 * row + 36), ya)
+        cp(o("CC", 24, 96), o("SB", 15, 1152, 16))
+        tt(o("DL"), o("CC", 0, 72), o("CC", 24, 96), OP.subtract)
+        for r in range(3):
+            tt(r3("E%d" % r, T["E%d" % r][:], 0, 3), r3("Y", T.Y[:, 0:3, 0:24], 0, 108), r3("Y", T.Y[:, r:r + 3, 12:36], 36 * r, 36 * r + 108), OP.is_equal)
+        tt(r3("E0", T.E0[:], 0, 3), r3("E0", T.E0[:], 0, 3), r3("E1", T.E1[:], 0, 3), OP.max)
+        tt(o("H"), r3("E0", T.E0[:], 0, 3), r3("E2", T.E2[:], 0, 3), OP.max)
+        tt(o("H", 24, 48), o("H", 0, 24), o("H", 24, 48), OP.max)
+        tt(o("H", 48, 72), o("H", 24, 48), o("H", 48, 72), OP.max)
+        tt(o("PRD"), o("DL"), o("H"), OP.mult)
+        tt(o("T1"), o("PRD", 0, 24), o("PRD", 24, 48), OP.add)
+        tt(o("T2"), o("PRD", 48, 72), o("CC", 72, 96), OP.add)
+        do("v", lambda: g.vector.tensor_tensor(T.QQ[:, 0, :, :], o("T1")[0], o("T2")[0], OP.add), [("QQ", 0, 24)], o("T1")[1] + o("T2")[1])
+        do("v", lambda: g.vector.tensor_copy(T.UAB[:], T.QQ[:, 0, :, :]), [("UAB", 0, 24)], [("QQ", 0, 24)])
+        cp(o("KL", 0, 192), ind("KDW", 0, V, "UAB", 0, 12))
+        act(o("XAB"), ind("XW", 0, V, "UAB", 0, 24))
+        mm(o("PXP", 0, 384), o("IDB"), o("XAB"), True, True)
+        for hf in range(2):
+            act(o("XA", 1536 * hf, 1536 * hf + 1536), ind("XW", 0, V, "KL", 96 * hf, 96 * hf + 96))
+        cp(o("KL", 192, 384), ind("KDW", 0, V, "UAB", 12, 24))
+        for hf in range(2):
+            act(o("XB", 1536 * hf, 1536 * hf + 1536), ind("XW", 0, V, "KL", 192 + 96 * hf, 288 + 96 * hf))
+        cp(r3("KF", T.KF[:], 0, 12), o("KL"))
+        for gp in range(2):
+            for cq in range(2):
+                mm((T.PMX[:, :, 16 * gp:16 * gp + 16], [("PMX", 0, 12)]), o("P%d%d" % (gp, cq)), (T.KF[:, :, cq, :], [("KF", 0, 12)]), cq == 0, cq == 1)
+        tt(o("PF", 0, 12), o("H", 0, 12), o("DL", 24, 36), OP.mult)
+        tt(o("PF", 12, 24), o("H", 24, 36), o("DL", 48, 60), OP.mult)
+        tt(o("F1"), o("PF", 0, 12), o("PF", 12, 24), OP.add)
+        tt(o("FW"), o("F1"), o("CC", 72, 84), OP.add)
+        tt(o("NE"), qq(0, 0), qq(0, 1), OP.not_equal)
+        tt(o("ME2", 0, 12), o("NE"), o("H", 48, 60), OP.mult)
+        tt(o("ME2", 12, 24), o("NE"), o("H", 48, 60), OP.mult)
+        ts(o("UN"), o("ME2", 0, 12), -1.0, OP.mult, 1.0, OP.add)
+        ts(o("THR"), o("ME2"), -4096.0, OP.mult, 4096.0 + 143.0, OP.add)
+        cp(o("FR"), ind("FAW", 0, V, "UAB", 0, 12))
+        for c in range(12):
+            ts(r3("EQ", T.EQ[:, c, 192 - 16 * c:208], c, c + 1), o("FR", 0, 16 * c + 16), o("FW", c, c + 1), OP.is_equal)
+        eqb = r3("EQ", T.EQ[:, :, 192:208], 0, 12)
+        tt(eqb, eqb, r3("TRI", T.TRI[:], 0, 12), OP.mult)
+        for c in range(12):
+            e = r3("EQ", T.EQ[:, c, 192 - 16 * c:208], c, c + 1)
+            scan(r3("EQS", T.EQS[:, c, 192 - 16 * c:208], c, c + 1), e, e, OP.max, OP.max)
+        ts(o("CM"), r3("EQS", T.EQS[:, :, 207], 0, 12), -1.0, OP.mult, 1.0, OP.add)
+        tt(o("CU"), o("CM"), o("UN"), OP.mult)
+        do("v", lambda: g.vector.transpose(T.KT[:], T.PMX[:]), [("KT", 0, 12)], [("PMX", 0, 12)])
+        if not last:
+            tt(o("G"), ind("KDW", 0, V, "UAB", 0, 24), o("MW"), OP.mult)
+            scan(o("SD"), o("RST"), o("G"), OP.mult, OP.add)
+            cp(qq(2), o("SD", 15, 384, 16))
+        for sd in range(2):
+            xn, mn, gn, pk = ("XA", "XB")[sd], ("MA", "MB")[sd], ("GA1", "GB1")[sd], ("PKA", "PKB")[sd]
+            for hf in range(2):
+                l0, l1 = 96 * hf, 96 * hf + 96
+                for j in range(16):
+                    tt(r3("%s_%d" % (mn, j), T[mn][:, l0:l1, j], l0, l1), o(xn, 16 * l0 + j, 16 * l1, 16), o("PXP", 192 * (1 - sd) + l0, 192 * (1 - sd) + l1), OP.max)
+                mm(o(pk, 96 * hf, 96 * hf + 96), o("IDB"), o("CJ", 0, 96), True, False)
+                for s in range(16):
+                    mm(o(pk, 96 * hf, 96 * hf + 96), o("LS", 128 * s, 128 * s + 128), (T[mn][:, l0 + s:l1:16, :], [("%s_%d" % (mn, j), l0, l1) for j in range(16)]), False, s == 15)
+                scan(o(gn, 16 * l0, 16 * l1), o("RSB", 16 * l0, 16 * l1), o(xn, 16 * l0, 16 * l1), OP.mult, OP.max)
+            scan(o("RUN"), o("RST", 0, 192), o(pk, 0, 192), OP.mult, OP.max)
+            tt(o("TT"), o("RUN"), o(pk, 0, 192), OP.subtract)
+            tt(o("DD"), r3("KT", T.KT[:, 6 * sd:6 * sd + 6, :], 6 * sd, 6 * sd + 6), o("TT"), OP.subtract)
+            scan(o("LSC"), o("TT"), o("DD"), OP.min, OP.max)
+            le = o("LSC", 15, 192, 16)
+            ts(o("UL3", 12 * sd, 12 * sd + 12), le, 4096.0, OP.mult)
+            cp(o("K2", 192 * sd, 192 * sd + 192), ind("KDW", 0, V, "UL3", 12 * sd, 12 * sd + 12))
+            ts(qq(1, sd), le, 4096.0, OP.mult)
+            if sd == 0:
+                ts(o("UL3", 24, 36), le, 4096.0, OP.mult)
+            if sd == 1 and not last:
+                act(o("LR"), ind("IOT", 0, V, "UL3", 0, 24))
+            for hf in range(2):
+                act(o(("YA", "YB")[sd], 1536 * hf, 1536 * hf + 1536), ind("XW", 0, V, "K2", 192 * sd + 96 * hf, 192 * sd + 96 * hf + 96))
+            if sd == 1:
+                act(o("FV"), ind("FAW", 0, V, "UL3", 12, 36))
+            for s in range(16):
+                kw = o("LW", 128 * s, 128 * s + 128)
+                if sd == 0:
+                    mm(o("PH", 0, 12), kw, o("GA1", 16 * s + 15, 3072, 256), s == 0, False)
+                if not last:
+                    mm(o("PS", 0, 3), kw, o(gn, 2304 + 16 * s + 15, 3072, 256), s == 0 and sd == 0, False)
+        lf = qq(1)
+        ts(o("ZF"), lf, float(Z), OP.is_equal)
+        tt(o("ZD"), qq(0), lf, OP.subtract)
+        tt(o("ZP"), o("ZD"), o("ZF"), OP.mult)
+        tt(qq(3), lf, o("ZP"), OP.add)
+        tt(o("NZ"), o("ZF", 0, 12), o("ZF", 12, 24), OP.max)
+        ts(o("NZ2"), o("NZ"), -1.0, OP.mult, 1.0, OP.add)
+        tt(o("CN"), o("CM"), o("NZ2"), OP.mult)
+        if last:
+            cp(qq(2), qq(1))
+        do("v", lambda: g.vector.tensor_tensor(T.QD[:], T.QQ[:, :, 1, :], T.QQ[:, :, 0, :], OP.subtract), [("QD", 0, 4)], [("QQ", 0, 96)])
+        do("v", lambda: g.vector.tensor_tensor(T.E4[:], T.QQ[:, 0:2, :, :], T.D4[:], OP.subtract), [("E4", 0, 48)], [("QQ", 0, 48), ("D4", 0, 48)])
+        for sd in range(2):
+            xn, gn = ("YA", "YB")[sd], ("GA2", "GB2")[sd]
+            for hf in range(2):
+                l0, l1 = 1536 * hf, 1536 * hf + 1536
+                scan(o(gn, l0, l1), o("RSB", l0, l1), o(xn, l0, l1), OP.mult, OP.max)
+            if sd == 0:
+                mm(o("PC", 0, 192), o("IHB"), o("GA1", 15, 3072, 16), True, False)
+                mm(o("PC", 0, 192), o("IHB"), o("GA2", 15, 3072, 16), False, True)
+                act(o("XW", UO, UO + 192), o("PC", 0, 192))
+            for s in range(16):
+                kw = o("LW", 128 * s, 128 * s + 128)
+                if sd == 0:
+                    mm(o("PH", 0, 12), kw, o("GA2", 16 * s + 15, 3072, 256), False, s == 15)
+                if not last and sd == 0:
+                    mm(o("PS", 0, 3), kw, o(gn, 2304 + 16 * s + 15, 3072, 256), False, False)
+            if sd == 0:
+                if not last:
+                    mm(o("PKA", 0, 384), o("IDF"), o("LR"), True, True)
+                    for h0 in (0, 192):
+                        mm(o("PXP", h0, h0 + 192), o("IDF"), o("LR", 192 - h0, 384 - h0), True, False)
+                        mm(o("PXP", h0, h0 + 192), o("NIF"), o("LR", h0, h0 + 192), False, True)
+                    tt(o("OH"), r3("KF", T.KF[:], 0, 12), o("PKA", 0, 384), OP.is_equal)
+                    tt(o("MM"), o("OH"), o("PXP", 0, 384), OP.mult)
+                    tt(o("NK"), r3("KF", T.KF[:], 0, 12), o("MM"), OP.add)
+                cp(o("HI"), o("PH", 0, 12))
+                ts(o("HJ"), o("HI"), 63, OP.bitwise_and)
+                ts(o("B2", 0, 12), o("E1C"), float(192 * rnd), OP.add)
+                tt(o("BS", 0, 12), o("B2", 0, 12), o("HJ"), OP.add)
+        mm(o("PD", 0, 192), o("IDB"), o("GA1", 15, 3072, 16), True, False)
+        mm(o("PD", 0, 192), o("NIB"), o("GB1", 15, 3072, 16), False, False)
+        mm(o("PD", 0, 192), o("IDB"), o("GA2", 15, 3072, 16), False, False)
+        mm(o("PD", 0, 192), o("NIB"), o("GB2", 15, 3072, 16), False, True)
+        if not last:
+            for s in range(16):
+                mm(o("PS", 0, 3), o("LW", 128 * s, 128 * s + 128), o("GB2", 2304 + 16 * s + 15, 3072, 256), False, s == 15)
+        ts(o("CMP", 0, 192), o("PD", 0, 192), 0.0, OP.is_gt)
+        ts(o("CMP", 192, 384), o("PD", 0, 192), 0.0, OP.is_lt)
+        for s in range(16):
+            mm(o("PC", 0, 24), o("LS", 128 * s, 128 * s + 128), o("CMP", s, 384, 16), s == 0, s == 15)
+        tt(o("WIN"), o("PC", 0, 24), o("THR"), OP.is_ge)
+        tt(o("WON"), o("WIN", 0, 12), o("WIN", 12, 24), OP.add)
+        for k in range(4):
+            tt(r3("QP", T.QP[:, k, :], k, k + 1), r3("QD", T.QD[:, k, :], k, k + 1), o("WIN", 12, 24), OP.mult)
+        do("v", lambda: g.vector.tensor_tensor(T.Q[:], T.QQ[:, :, 0, :], T.QP[:], OP.add), [("Q", 0, 48)], [("QQ", 0, 96), ("QP", 0, 4)])
+        tt(o("SW"), o("CN"), o("WON"), OP.mult)
+        for k in range(4):
+            tt(r3("EP", T.EP[:, k, :], k, k + 1), o("E4", 12 * k, 12 * k + 12), o("SW"), OP.mult)
+        do("v", lambda: g.vector.tensor_tensor(T.DS[:], T.D4[:], T.EP[:], OP.add), [("DS", 0, 48)], [("D4", 0, 48), ("EP", 0, 4)])
+        cp(o("DU"), o("DS"))
+        tt(o("B2"), o("Q", 0, 24), o("BS"), OP.subtract)
+        tt(o("B3"), o("B2"), o("ME2"), OP.mult)
+        tt(o("B2"), o("BS"), o("B3"), OP.add)
+        cp(o("EU"), o("B2"))
+        xe = RT + 192 * rnd + 192
+        act(o("XE"), ind("XW", 0, xe, "EU", 12, 24))
+        tt(o("OK1"), o("CM"), o("WON"), OP.mult)
+        tt(o("OK2"), o("OK1"), o("CU"), OP.add)
+        tt(o("DX"), o("Q", 0, 12), o("XD"), OP.subtract)
+        tt(o("DX2"), o("DX"), o("OK2"), OP.mult)
+        tt(o("DX"), o("XD"), o("DX2"), OP.add)
+        cp(o("XU"), o("DX"))
+        cp(scat("FAW", 0, 2176, "DU", 24, 48), o("FV"))
+        if last:
+            dma("s", T.YFA[:], T.FAW[0:128:16, 0:V], [("YFA", 0, 112)], [("FAW", 0, V)])
+        tt(o("XS"), ind("XW", 0, xe, "EU", 0, 12), o("XE"), OP.add)
+        ts(o("XN"), o("XS"), 0.5, OP.mult, -0.375, OP.add)
+        cp(scat("XW", 0, RT, "XU", 0, 12), o("XN"))
+        if last:
+            dma("gq", T.yx[:], T.XW[:, 0:V], [("yx", 0, V)], [("XW", 0, V)])
+            tt(o("YFB"), o("YFA"), o("DPF"), OP.subtract)
+            dma("s", T.yf[:], T.YFB[:], [("yf", 0, V)], [("YFB", 0, 112)])
+            break
+        send(rnd + 1)
+        tt(o("SI"), o("PS", 0, 3), o("SL"), OP.add)
+        ts(o("SJ"), o("SI"), 2047, OP.bitwise_and)
+        ts(o("SF"), o("SJ"), float(V), OP.is_ge, float(V), OP.mult)
+        cp(o("CC", 0, 12), o("Q", 36, 48))
+        cp(o("CC", 12, 21), o("Q", 24, 33))
+        tt(o("CC", 21, 24), o("SJ"), o("SF"), OP.subtract)
+        cp(o("U0"), o("CC", 0, 24))
+        cp(scat("KDW", 0, 2176, "DU", 0, 24), o("NK"))
+    for s, n in total.items():
+        if waited.get(s, 0) < n:
+            g.wait_ge(T.sem[s], n)

@@ -7,6 +7,10 @@ XC = RT + 192 * RO
 f, b, i4, u2 = "float32", "bfloat16", "int32", "uint16"
 
 
+VL = 144
+PE_HALVES = (1,)
+
+
 def S_(shape, d):
     return ("sbuf", shape, d)
 
@@ -33,7 +37,7 @@ SCRATCH = {
     "E0": S_([128, 3, 24], f), "E1": S_([128, 3, 24], f), "E2": S_([128, 3, 24], f), "H": S_([128, 72], f),
     "DL": S_([128, 72], f), "PRD": S_([128, 72], f), "T1": S_([128, 24], f), "T2": S_([128, 24], f),
     "PF": S_([128, 24], f), "F1": S_([128, 12], f), "FW": S_([128, 12], f),
-    "QQ": S_([128, 4, 2, 12], f), "QD": S_([128, 4, 12], f), "QP": S_([128, 4, 12], f), "Q": S_([128, 48], f),
+    "QQ": S_([128, 4, 2, 12], f), "QD": S_([128, 48], f), "QP": S_([128, 48], f), "Q": S_([128, 48], f),
     "UAB": S_([128, 24], u2), "NE": S_([128, 12], f), "ME2": S_([128, 24], f), "UN": S_([128, 12], f), "THR": S_([128, 24], f),
     "KL": S_([128, 384], u2), "KF": S_([128, 12, 2, 16], f), "KT": S_([128, 12, 32], f), "SD": S_([128, 384], f),
     "XAB": S_([128, 384], b), "FR": S_([128, 192], u2), "CM": S_([128, 12], f), "CU": S_([128, 12], f), "CN": S_([128, 12], f),
@@ -43,18 +47,19 @@ SCRATCH = {
     "RUN": S_([128, 192], f), "TT": S_([128, 192], f), "DD": S_([128, 192], f), "LSC": S_([128, 192], f),
     "UL3": S_([128, 36], u2), "K2": S_([128, 384], u2), "ZF": S_([128, 24], f), "ZD": S_([128, 24], f), "ZP": S_([128, 24], f),
     "NZ": S_([128, 12], f), "NZ2": S_([128, 12], f), "LR": S_([128, 384], f), "OH": S_([128, 384], f), "MM": S_([128, 384], f),
-    "NK": S_([128, 384], i4), "FV": S_([128, 384], f), "CMP": S_([128, 384], b), "WIN": S_([128, 24], f), "WON": S_([128, 12], f),
-    "SW": S_([128, 12], f), "E4": S_([128, 48], f), "EP": S_([128, 4, 12], f), "DS": S_([128, 48], f), "DU": S_([128, 48], u2),
+    "NK": S_([128, 384], i4), "FV": S_([128, 384], f), "CMP": S_([128, 384], b), "WON": S_([128, 12], f),
+    "E4": S_([128, 48], f), "EP": S_([128, 48], f), "DS": S_([128, 48], f), "DU": S_([128, 48], u2),
     "HI": S_([128, 12], i4), "HJ": S_([128, 12], i4), "BS": S_([128, 24], f), "B2": S_([128, 24], f), "B3": S_([128, 24], f),
     "EU": S_([128, 24], u2), "OK1": S_([128, 12], f), "OK2": S_([128, 12], f), "DX": S_([128, 12], f), "DX2": S_([128, 12], f),
     "XU": S_([128, 12], u2), "XE": S_([128, 192], f), "XS": S_([128, 192], f), "XN": S_([128, 192], i4),
-    "SI": S_([128, 3], i4), "SJ": S_([128, 3], i4), "SF": S_([128, 3], f),
-    "RB": S_([128, 64 * RO], f),
+    "SI": S_([128, 3], i4), "SJ": S_([128, 3], i4), "SF": S_([128, 3], f), "SH": S_([128, 3], f),
+    "RB": S_([128, 64 * RO], f), "N12": S_([128, 4], i4), "M12": S_([128, 3], f), "R12": S_([128, 3], f),
+    "LQ": S_([128, 4], u2), "LE": S_([128, 4], u2), "WB": S_([128, 40], f),
 }
 for _n in ("PXP", "PMX", "PKA", "PKB", "PD", "PC", "PH", "PS"):
     SCRATCH[_n] = ("psum", [128, 512], f)
 SMALL, _w = {}, 0
-for _n in ("PMF L16 LN KTF KT3 E1C XD SL T1 T2 PF F1 FW NE ME2 UN THR CM CU CN ZF ZD ZP NZ NZ2 WIN WON SW BS B2 B3 "
+for _n in ("PMF L16 LN KTF KT3 E1C XD SL T1 T2 PF F1 FW NE ME2 UN THR CM CU CN ZF ZD ZP NZ NZ2 M12 R12 WON BS B2 B3 "
            "OK1 OK2 DX DX2 SF WTF").split():
     SMALL[_n] = (_w, SCRATCH[_n][1][1])
     _w += (SCRATCH[_n][1][1] + 3) // 4 * 4
@@ -245,6 +250,8 @@ def rank_program(g, core, T, topo):
     dma("s", T.KDW[:, 0:V], T.kd[:], [("KDW", 0, V)], [])
 
     ms(o("ONE"), 1.0)
+    ms(o("RST"), 1.0)
+    ms(o("RST", 0, 384, 16), 0.0)
     asel(o("MGT"), o("ONE"), [[1, 128]], OP.is_ge, 0, -16)
     asel(o("B8"), o("MGT"), [[-1, 128]], OP.is_ge, 15, 16)
     asel(o("IDF"), o("ONE"), [[-1, 128]], OP.is_equal, 0, 1)
@@ -255,7 +262,8 @@ def rank_program(g, core, T, topo):
         q = "s" if k % 2 == 0 else "a"
         dma(q, T.FAW[k:128:16, 0:V], T.FAD[:], [("FAW%d" % k, 0, V)], [("FAD", 0, V)], sem="d18" if q == "s" else "d19")
     acc["FAW"] = [(0, V, True, "d18", 128, "dma"), (0, V, True, "d19", 128, "dma")]
-    send(0)
+    ms(o("RSB"), 1.0)
+    ms(o("RSB", 0, 3072, 16), 0.0)
     ms(o("PR0"), 0.0)
     ms(o("PR1"), 0.0)
     for k in range(4):
@@ -272,44 +280,56 @@ def rank_program(g, core, T, topo):
     asel(o("P01"), o("PR1"), [[-1, 128]], OP.is_equal, 16, 1)
     asel(o("P10"), o("PR0"), [[-1, 128]], OP.is_equal, -16, 1)
     iota(o("IOT"), [[1, V]], 0, 0)
+    send(0)
     tt(o("D64"), o("IDF", 0, 64), o("IDF", 64, 128), OP.add)
     tt(o("D32"), o("D64", 0, 32), o("D64", 32, 64), OP.add)
     tt(o("MW", 0, 16), o("D32", 0, 16), o("D32", 16, 32), OP.add)
     for a0, n in ((16, 16), (32, 32), (64, 64), (128, 128), (256, 128)):
         cp(o("MW", a0, a0 + n), o("MW", 0, n))
-    ms(o("RST"), 1.0)
-    ms(o("RST", 0, 384, 16), 0.0)
     do("v", lambda: g.vector.tensor_copy(T.PAF[0:8, :], T.PAI[0:8, :]), [("PAF", 0, 384)], [("PAI", 0, 384)])
     do("p", lambda: g.tensor.matmul(T.PC[:, 0:384], T.B8[0:8, :], T.PAF[0:8, :], True, True), [("PC", 0, 384)], [("B8", 0, 128), ("PAF", 0, 384)])
     tt(o("G"), o("PC", 0, 384), o("MW"), OP.mult)
     scan(o("SD"), o("RST"), o("G"), OP.mult, OP.add)
     cp(o("U0"), o("SD", 15, 384, 16))
     cp(o("CC", 0, 24), o("SD", 15, 384, 16))
-    ts(o("PMJ"), o("PMI"), 15, OP.bitwise_and)
-    cp(o("PMF"), o("PMJ"))
-    ts(o("LN"), o("L16"), o("PMF"), OP.add)
-    ts(o("KTI"), o("LN"), 1.0 / 3, OP.mult, -1.0 / 3, OP.add)
-    ts(o("KTF"), o("KTI"), -3.0, OP.mult)
-    tt(o("KT3"), o("LN"), o("KTF"), OP.add)
-    ts(o("E1C"), o("KT3"), 64.0, OP.mult, float(RT), OP.add)
-    ts(o("XD"), o("LN"), float(DO), OP.add)
-    for k in range(4):
-        ts(o("D4", 12 * k, 12 * k + 12), o("LN"), float(V + 192 * (k % 2)), OP.add)
-    ts(o("BS", 12, 24), o("LN"), float(UO), OP.add)
-    ts(o("SL"), o("LN", 9, 12), 977.0, OP.mult)
-    ms(o("RSB"), 1.0)
-    ms(o("RSB", 0, 3072, 16), 0.0)
-    do("v", lambda: g.vector.tensor_scalar(T.TRI[:], T.TIN[:], o("PMF")[0], None, OP.is_lt), [("TRI", 0, 12)], [("TIN", 0, 192)] + o("PMF")[1])
     ms(o("LS"), 0.0)
-    for s in range(16):
-        ts(o("LS", 128 * s + s, 128 * s + 128, 16), o("MG", 0, 128, 16), 16.0, OP.mult)
-    ts(o("WTF"), o("WTI"), 1.0 / 16, OP.mult)
-    ts(o("LW"), o("LS"), o("WTF"), OP.mult)
+    ms(o("XW", V, RT), 0.0)
     cp(o("IDB"), o("IDF"))
     ts(o("NIB"), o("IDF"), -1.0, OP.mult)
-    ts(o("IHB"), o("IDF"), 0.5, OP.mult)
-    ts(o("NIF"), o("IDF"), -1.0, OP.mult)
-    ms(o("XW", V, RT), 0.0)
+    ts(o("PMJ"), o("PMI"), 15, OP.bitwise_and)
+    cp(o("PMF"), o("PMJ"))
+    for s in range(16):
+        ts(o("LS", 128 * s + s, 128 * s + 128, 16), o("MG", 0, 128, 16), 16.0, OP.mult)
+    ts(o("LN"), o("L16"), o("PMF"), OP.add)
+
+    fill = []
+
+    def step(n=1):
+        for _ in range(min(n, len(fill))):
+            fill.pop(0)()
+
+    def twelfths(lst, ofs):
+        ts(o("N12", 0, 3), o("LN", 0, 3), 1.0 / 12, OP.mult, -11.0 / 24, OP.add)
+        ts(o("M12"), o("N12", 0, 3), -12.0, OP.mult, float(ofs), OP.add)
+        tt(o("R12"), o("LN", 0, 3), o("M12"), OP.add)
+        cp(o(lst, 0, 3), o("R12"))
+    fill += [
+        lambda: do("v", lambda: g.vector.tensor_scalar(T.TRI[:], T.TIN[:], o("PMF")[0], None, OP.is_lt), [("TRI", 0, 12)], [("TIN", 0, 192)] + o("PMF")[1]),
+        lambda: ts(o("WTF"), o("WTI"), 1.0 / 16, OP.mult),
+        lambda: ts(o("LW"), o("LS"), o("WTF"), OP.mult),
+        lambda: ts(o("IHB"), o("IDF"), 0.5, OP.mult),
+        lambda: ts(o("NIF"), o("IDF"), -1.0, OP.mult),
+        lambda: ts(o("KTI"), o("LN"), 1.0 / 3, OP.mult, -1.0 / 3, OP.add),
+        lambda: ts(o("XD"), o("LN"), float(DO), OP.add),
+        lambda: ts(o("KTF"), o("KTI"), -3.0, OP.mult),
+        lambda: ts(o("BS", 12, 24), o("LN"), float(UO), OP.add),
+        lambda: tt(o("KT3"), o("LN"), o("KTF"), OP.add),
+        lambda: ts(o("SL"), o("LN", 9, 12), 977.0, OP.mult),
+        lambda: ts(o("E1C"), o("KT3"), 64.0, OP.mult, float(RT), OP.add),
+        lambda: twelfths("LQ", 12),
+        lambda: twelfths("LE", 24)]
+    for k in range(4):
+        fill.append(lambda k=k: ts(o("D4", 12 * k, 12 * k + 12), o("LN"), float(V + 192 * (k % 2)), OP.add))
 
     def r3(n, ap, lo, hi):
         return ap, [(n, lo, hi)]
@@ -323,11 +343,14 @@ def rank_program(g, core, T, topo):
         last = rnd == RO - 1
         for k in range(3):
             tt(o("G"), ind("FAW", 0, V, "U%d" % k, 0, 24), o("MW"), OP.mult)
+            step()
             scan(o("SB", 384 * k, 384 * k + 384), o("RST"), o("G"), OP.mult, OP.add)
             y = o("SB", 384 * k + 15, 384 * k + 384, 16)
             ya = o("SB", 384 * k + 15, 384 * k + 192, 16)
+            step()
             if k < 2:
                 cp(o("U%d" % (k + 1)), y)
+            step()
             for row in ((k, k + 3) if k < 2 else (k,)):
                 act(r3("Y", T.Y[:, row, 0:24], 36 * row, 36 * row + 24), y)
                 act(r3("Y", T.Y[:, row, 24:36], 36 * row + 24, 36 * row + 36), ya)
@@ -336,9 +359,13 @@ def rank_program(g, core, T, topo):
         for r in range(3):
             tt(r3("E%d" % r, T["E%d" % r][:], 0, 3), r3("Y", T.Y[:, 0:3, 0:24], 0, 108), r3("Y", T.Y[:, r:r + 3, 12:36], 36 * r, 36 * r + 108), OP.is_equal)
         tt(r3("E0", T.E0[:], 0, 3), r3("E0", T.E0[:], 0, 3), r3("E1", T.E1[:], 0, 3), OP.max)
+        step(2)
         tt(o("H"), r3("E0", T.E0[:], 0, 3), r3("E2", T.E2[:], 0, 3), OP.max)
+        step()
         tt(o("H", 24, 48), o("H", 0, 24), o("H", 24, 48), OP.max)
+        step()
         tt(o("H", 48, 72), o("H", 24, 48), o("H", 48, 72), OP.max)
+        step(len(fill))
         tt(o("PRD"), o("DL"), o("H"), OP.mult)
         tt(o("T1"), o("PRD", 0, 24), o("PRD", 24, 48), OP.add)
         tt(o("T2"), o("PRD", 48, 72), o("CC", 72, 96), OP.add)
@@ -368,28 +395,41 @@ def rank_program(g, core, T, topo):
         cp(o("FR"), ind("FAW", 0, V, "UAB", 0, 12))
         for c in range(12):
             ts(r3("EQ", T.EQ[:, c, 192 - 16 * c:208], c, c + 1), o("FR", 0, 16 * c + 16), o("FW", c, c + 1), OP.is_equal)
-        eqb = r3("EQ", T.EQ[:, :, 192:208], 0, 12)
-        tt(eqb, eqb, r3("TRI", T.TRI[:], 0, 12), OP.mult)
-        for c in range(12):
-            e = r3("EQ", T.EQ[:, c, 192 - 16 * c:208], c, c + 1)
-            scan(r3("EQS", T.EQS[:, c, 192 - 16 * c:208], c, c + 1), e, e, OP.max, OP.max)
-        ts(o("CM"), r3("EQS", T.EQS[:, :, 207], 0, 12), -1.0, OP.mult, 1.0, OP.add)
-        tt(o("CU"), o("CM"), o("UN"), OP.mult)
-        do("v", lambda: g.vector.transpose(T.KT[:], T.PMX[:]), [("KT", 0, 12)], [("PMX", 0, 12)])
-        if not last:
-            tt(o("G"), ind("KDW", 0, V, "UAB", 0, 24), o("MW"), OP.mult)
-            scan(o("SD"), o("RST"), o("G"), OP.mult, OP.add)
-            cp(qq(2), o("SD", 15, 384, 16))
         for sd in range(2):
             xn, mn, gn, pk = ("XA", "XB")[sd], ("MA", "MB")[sd], ("GA1", "GB1")[sd], ("PKA", "PKB")[sd]
             for hf in range(2):
                 l0, l1 = 96 * hf, 96 * hf + 96
-                for j in range(16):
+                for j in range(0 if sd and hf in PE_HALVES else 16):
                     tt(r3("%s_%d" % (mn, j), T[mn][:, l0:l1, j], l0, l1), o(xn, 16 * l0 + j, 16 * l1, 16), o("PXP", 192 * (1 - sd) + l0, 192 * (1 - sd) + l1), OP.max)
                 mm(o(pk, 96 * hf, 96 * hf + 96), o("IDB"), o("CJ", 0, 96), True, False)
                 for s in range(16):
                     mm(o(pk, 96 * hf, 96 * hf + 96), o("LS", 128 * s, 128 * s + 128), (T[mn][:, l0 + s:l1:16, :], [("%s_%d" % (mn, j), l0, l1) for j in range(16)]), False, s == 15)
                 scan(o(gn, 16 * l0, 16 * l1), o("RSB", 16 * l0, 16 * l1), o(xn, 16 * l0, 16 * l1), OP.mult, OP.max)
+            for hf in (() if sd else PE_HALVES):
+                l0, l1 = 96 * hf, 96 * hf + 96
+                for j4 in range(4):
+                    pb = ("PD", "PC", "PH", "PS")[j4]
+                    for j in range(4):
+                        po = o(pb, j, 384, 4)
+                        mm(po, o("IDB"), o("XB", 16 * l0 + 4 * j4 + j, 16 * l1, 16), True, False)
+                        mm(po, o("NIB"), o("XAB", l0, l1), False, True)
+                    do("a", lambda: g.scalar.activation(T.MB[:, l0:l1, 4 * j4:4 * j4 + 4], T[pb][:, 0:384], AF.Relu),
+                       [("MB_%d" % (4 * j4 + j), l0, l1) for j in range(4)], [(pb, 0, 384)])
+            if sd == 0:
+                do("v", lambda: g.vector.transpose(T.KT[:], T.PMX[:]), [("KT", 0, 12)], [("PMX", 0, 12)])
+                if not last:
+                    tt(o("G"), ind("KDW", 0, V, "UAB", 0, 24), o("MW"), OP.mult)
+            else:
+                eqb = r3("EQ", T.EQ[:, :, 192:208], 0, 12)
+                tt(eqb, eqb, r3("TRI", T.TRI[:], 0, 12), OP.mult)
+                if not last:
+                    scan(o("SD"), o("RST"), o("G"), OP.mult, OP.add)
+                for c in range(12):
+                    e = r3("EQ", T.EQ[:, c, 192 - 16 * c:208], c, c + 1)
+                    scan(r3("EQS", T.EQS[:, c, 192 - 16 * c:208], c, c + 1), e, e, OP.max, OP.max)
+                if not last:
+                    act(qq(2), o("SD", 15, 384, 16))
+                ts(o("CM"), r3("EQS", T.EQS[:, :, 207], 0, 12), -1.0, OP.mult, 1.0, OP.add)
             scan(o("RUN"), o("RST", 0, 192), o(pk, 0, 192), OP.mult, OP.max)
             tt(o("TT"), o("RUN"), o(pk, 0, 192), OP.subtract)
             tt(o("DD"), r3("KT", T.KT[:, 6 * sd:6 * sd + 6, :], 6 * sd, 6 * sd + 6), o("TT"), OP.subtract)
@@ -400,29 +440,34 @@ def rank_program(g, core, T, topo):
             ts(qq(1, sd), le, 4096.0, OP.mult)
             if sd == 0:
                 ts(o("UL3", 24, 36), le, 4096.0, OP.mult)
-            if sd == 1 and not last:
-                act(o("LR"), ind("IOT", 0, V, "UL3", 0, 24))
-            for hf in range(2):
-                act(o(("YA", "YB")[sd], 1536 * hf, 1536 * hf + 1536), ind("XW", 0, V, "K2", 192 * sd + 96 * hf, 192 * sd + 96 * hf + 96))
-            if sd == 1:
-                act(o("FV"), ind("FAW", 0, V, "UL3", 12, 36))
-            for s in range(16):
-                kw = o("LW", 128 * s, 128 * s + 128)
-                if sd == 0:
-                    mm(o("PH", 0, 12), kw, o("GA1", 16 * s + 15, 3072, 256), s == 0, False)
+            k2 = 192 * sd
+            act(o(("YA", "YB")[sd], 0, 1536), ind("XW", 0, V, "K2", k2, k2 + 96))
+            if sd == 0:
+                act(o("YA", 1536, 3072), ind("XW", 0, V, "K2", 96, 192))
+            else:
+                act(o("YB", 1536, 16 * VL), ind("XW", 0, V, "K2", 288, 192 + VL))
+                if VL < 192:
+                    cp(o("YB", 16 * VL, 3072), ind("XW", 0, V, "K2", 192 + VL, 384))
+                tt(o("CU"), o("CM"), o("UN"), OP.mult)
                 if not last:
-                    mm(o("PS", 0, 3), kw, o(gn, 2304 + 16 * s + 15, 3072, 256), s == 0 and sd == 0, False)
+                    act(o("LR"), ind("IOT", 0, V, "UL3", 0, 24))
+                act(o("FV"), ind("FAW", 0, V, "UL3", 12, 36))
+        for s in range(16):
+            kw = o("LW", 128 * s, 128 * s + 128)
+            mm(o("PH", 0, 12), kw, o("GA1", 16 * s + 15, 3072, 256), s == 0, False)
+            if not last:
+                mm(o("PS", 0, 3), kw, o("GB1", 2304 + 16 * s + 15, 3072, 256), s == 0, False)
         lf = qq(1)
         ts(o("ZF"), lf, float(Z), OP.is_equal)
         tt(o("ZD"), qq(0), lf, OP.subtract)
-        tt(o("ZP"), o("ZD"), o("ZF"), OP.mult)
-        tt(qq(3), lf, o("ZP"), OP.add)
         tt(o("NZ"), o("ZF", 0, 12), o("ZF", 12, 24), OP.max)
+        tt(o("ZP"), o("ZD"), o("ZF"), OP.mult)
         ts(o("NZ2"), o("NZ"), -1.0, OP.mult, 1.0, OP.add)
+        tt(qq(3), lf, o("ZP"), OP.add)
         tt(o("CN"), o("CM"), o("NZ2"), OP.mult)
         if last:
             cp(qq(2), qq(1))
-        do("v", lambda: g.vector.tensor_tensor(T.QD[:], T.QQ[:, :, 1, :], T.QQ[:, :, 0, :], OP.subtract), [("QD", 0, 4)], [("QQ", 0, 96)])
+        do("v", lambda: g.vector.tensor_tensor(T.QD[:], T.QQ[:, :, 1, :], T.QQ[:, :, 0, :], OP.subtract), [("QD", 0, 48)], [("QQ", 0, 96)])
         do("v", lambda: g.vector.tensor_tensor(T.E4[:], T.QQ[:, 0:2, :, :], T.D4[:], OP.subtract), [("E4", 0, 48)], [("QQ", 0, 48), ("D4", 0, 48)])
         for sd in range(2):
             xn, gn = ("YA", "YB")[sd], ("GA2", "GB2")[sd]
@@ -437,21 +482,6 @@ def rank_program(g, core, T, topo):
                 kw = o("LW", 128 * s, 128 * s + 128)
                 if sd == 0:
                     mm(o("PH", 0, 12), kw, o("GA2", 16 * s + 15, 3072, 256), False, s == 15)
-                if not last and sd == 0:
-                    mm(o("PS", 0, 3), kw, o(gn, 2304 + 16 * s + 15, 3072, 256), False, False)
-            if sd == 0:
-                if not last:
-                    mm(o("PKA", 0, 384), o("IDF"), o("LR"), True, True)
-                    for h0 in (0, 192):
-                        mm(o("PXP", h0, h0 + 192), o("IDF"), o("LR", 192 - h0, 384 - h0), True, False)
-                        mm(o("PXP", h0, h0 + 192), o("NIF"), o("LR", h0, h0 + 192), False, True)
-                    tt(o("OH"), r3("KF", T.KF[:], 0, 12), o("PKA", 0, 384), OP.is_equal)
-                    tt(o("MM"), o("OH"), o("PXP", 0, 384), OP.mult)
-                    tt(o("NK"), r3("KF", T.KF[:], 0, 12), o("MM"), OP.add)
-                cp(o("HI"), o("PH", 0, 12))
-                ts(o("HJ"), o("HI"), 63, OP.bitwise_and)
-                ts(o("B2", 0, 12), o("E1C"), float(192 * rnd), OP.add)
-                tt(o("BS", 0, 12), o("B2", 0, 12), o("HJ"), OP.add)
         mm(o("PD", 0, 192), o("IDB"), o("GA1", 15, 3072, 16), True, False)
         mm(o("PD", 0, 192), o("NIB"), o("GB1", 15, 3072, 16), False, False)
         mm(o("PD", 0, 192), o("IDB"), o("GA2", 15, 3072, 16), False, False)
@@ -463,48 +493,77 @@ def rank_program(g, core, T, topo):
         ts(o("CMP", 192, 384), o("PD", 0, 192), 0.0, OP.is_lt)
         for s in range(16):
             mm(o("PC", 0, 24), o("LS", 128 * s, 128 * s + 128), o("CMP", s, 384, 16), s == 0, s == 15)
-        tt(o("WIN"), o("PC", 0, 24), o("THR"), OP.is_ge)
-        tt(o("WON"), o("WIN", 0, 12), o("WIN", 12, 24), OP.add)
-        for k in range(4):
-            tt(r3("QP", T.QP[:, k, :], k, k + 1), r3("QD", T.QD[:, k, :], k, k + 1), o("WIN", 12, 24), OP.mult)
-        do("v", lambda: g.vector.tensor_tensor(T.Q[:], T.QQ[:, :, 0, :], T.QP[:], OP.add), [("Q", 0, 48)], [("QQ", 0, 96), ("QP", 0, 4)])
-        tt(o("SW"), o("CN"), o("WON"), OP.mult)
-        for k in range(4):
-            tt(r3("EP", T.EP[:, k, :], k, k + 1), o("E4", 12 * k, 12 * k + 12), o("SW"), OP.mult)
-        do("v", lambda: g.vector.tensor_tensor(T.DS[:], T.D4[:], T.EP[:], OP.add), [("DS", 0, 48)], [("D4", 0, 48), ("EP", 0, 4)])
-        cp(o("DU"), o("DS"))
-        tt(o("B2"), o("Q", 0, 24), o("BS"), OP.subtract)
-        tt(o("B3"), o("B2"), o("ME2"), OP.mult)
-        tt(o("B2"), o("BS"), o("B3"), OP.add)
-        cp(o("EU"), o("B2"))
+        cp(o("HI"), o("PH", 0, 12))
+        ts(o("B2", 0, 12), o("E1C"), float(192 * rnd), OP.add)
+        ts(o("HJ"), o("HI"), 63, OP.bitwise_and)
+        if not last:
+            tt(o("SH"), o("HI", 9, 12), o("SL"), OP.add)
+        tt(o("BS", 0, 12), o("B2", 0, 12), o("HJ"), OP.add)
+        tt(o("WB", 0, 24), o("PC", 0, 24), o("THR"), OP.is_ge)
         xe = RT + 192 * rnd + 192
+
+        def new_x(xe=xe, last=last):
+            return [
+                lambda: tt(o("OK1"), o("CM"), o("WON"), OP.mult),
+                lambda: tt(o("DX"), o("Q", 0, 12), o("XD"), OP.subtract),
+                lambda: tt(o("OK2"), o("OK1"), o("CU"), OP.add),
+                lambda: tt(o("XS"), ind("XW", 0, xe, "EU", 0, 12), o("XE"), OP.add),
+                lambda: tt(o("DX2"), o("DX"), o("OK2"), OP.mult),
+                lambda: ts(o("XN"), o("XS"), 0.5, OP.mult, -0.375, OP.add),
+                lambda: tt(o("DX"), o("XD"), o("DX2"), OP.add),
+                lambda: None if last else cp(scat("KDW", 0, 2176, "DU", 0, 24), o("NK")),
+                lambda: cp(o("XU"), o("DX")),
+                lambda: cp(scat("XW", 0, RT, "XU", 0, 12), o("XN"))]
+
+        def new_k():
+            def half(h0):
+                tt(o("NK", 32 * h0, 32 * h0 + 192), r3("KF", T.KF[:, h0:h0 + 6, :, :], h0, h0 + 6), o("MM", 32 * h0, 32 * h0 + 192),
+                   OP.subtract if h0 else OP.add)
+            return [
+                lambda: tt(o("OH"), r3("KF", T.KF[:], 0, 12), o("LR"), OP.is_equal),
+                lambda: tt(o("MM", 0, 192), o("OH", 0, 192), o("PKA", 0, 192), OP.mult),
+                lambda: tt(o("MM", 192, 384), o("OH", 192, 384), o("PKA", 0, 192), OP.mult),
+                lambda: half(0),
+                lambda: half(6)]
+
+        if not last:
+            mm(o("PKA", 0, 192), o("IDF"), o("LR", 192, 384), True, False)
+            mm(o("PKA", 0, 192), o("NIF"), o("LR", 0, 192), False, True)
+        tt(o("WON"), o("WB", 0, 12), o("WB", 12, 24), OP.add)
+        tt(o("QP"), ind("WB", 0, 24, "LQ", 0, 3), o("QD"), OP.mult)
+        tt(o("WB", 24, 36), o("CN"), o("WON"), OP.mult)
+        do("v", lambda: g.vector.tensor_tensor(T.Q[:], T.QQ[:, :, 0, :], T.QP[:], OP.add), [("Q", 0, 48)], [("QQ", 0, 96), ("QP", 0, 48)])
+        tt(o("EP"), ind("WB", 0, 36, "LE", 0, 3), o("E4"), OP.mult)
+        tt(o("B2"), o("Q", 0, 24), o("BS"), OP.subtract)
+        tt(o("DS"), o("D4"), o("EP"), OP.add)
+        tt(o("B3"), o("B2"), o("ME2"), OP.mult)
+        if not last:
+            tt(o("SI"), o("PS", 0, 3), o("SH"), OP.add)
+        cp(o("DU"), o("DS"))
+        tt(o("B2"), o("BS"), o("B3"), OP.add)
+        if not last:
+            ts(o("SJ"), o("SI"), 2047, OP.bitwise_and)
+        cp(o("EU"), o("B2"))
         act(o("XE"), ind("XW", 0, xe, "EU", 12, 24))
-        tt(o("OK1"), o("CM"), o("WON"), OP.mult)
-        tt(o("OK2"), o("OK1"), o("CU"), OP.add)
-        tt(o("DX"), o("Q", 0, 12), o("XD"), OP.subtract)
-        tt(o("DX2"), o("DX"), o("OK2"), OP.mult)
-        tt(o("DX"), o("XD"), o("DX2"), OP.add)
-        cp(o("XU"), o("DX"))
-        cp(scat("FAW", 0, 2176, "DU", 24, 48), o("FV"))
         if last:
+            ops = new_x()
+            for p in ops[:3]:
+                p()
+            cp(scat("FAW", 0, 2176, "DU", 24, 48), o("FV"))
             dma("s", T.YFA[:], T.FAW[0:128:16, 0:V], [("YFA", 0, 112)], [("FAW", 0, V)])
-        tt(o("XS"), ind("XW", 0, xe, "EU", 0, 12), o("XE"), OP.add)
-        ts(o("XN"), o("XS"), 0.5, OP.mult, -0.375, OP.add)
-        cp(scat("XW", 0, RT, "XU", 0, 12), o("XN"))
-        if last:
+            for p in ops[3:]:
+                p()
             dma("gq", T.yx[:], T.XW[:, 0:V], [("yx", 0, V)], [("XW", 0, V)])
             tt(o("YFB"), o("YFA"), o("DPF"), OP.subtract)
             dma("s", T.yf[:], T.YFB[:], [("yf", 0, V)], [("YFB", 0, 112)])
             break
-        send(rnd + 1)
-        tt(o("SI"), o("PS", 0, 3), o("SL"), OP.add)
-        ts(o("SJ"), o("SI"), 2047, OP.bitwise_and)
-        ts(o("SF"), o("SJ"), float(V), OP.is_ge, float(V), OP.mult)
         cp(o("CC", 0, 12), o("Q", 36, 48))
+        ts(o("SF"), o("SJ"), float(V), OP.is_ge, float(V), OP.mult)
         cp(o("CC", 12, 21), o("Q", 24, 33))
         tt(o("CC", 21, 24), o("SJ"), o("SF"), OP.subtract)
+        cp(scat("FAW", 0, 2176, "DU", 24, 48), o("FV"))
         cp(o("U0"), o("CC", 0, 24))
-        cp(scat("KDW", 0, 2176, "DU", 0, 24), o("NK"))
+        fill += new_k() + new_x() + [lambda rnd=rnd: send(rnd + 1)]
     for s, n in total.items():
         if waited.get(s, 0) < n:
             g.wait_ge(T.sem[s], n)

@@ -7,8 +7,10 @@ XC = RT + 192 * RO
 f, b, i4, u2 = "float32", "bfloat16", "int32", "uint16"
 
 
-VL = 144
-PE_HALVES = (1,)
+VL = 128
+NEQ = 4
+PARTS = ((0, 96), (96, 192))
+PE_HALVES = (0,)
 
 
 def S_(shape, d):
@@ -27,9 +29,10 @@ SCRATCH = {
     "MGT": S_([128, 128], f), "MG": S_([128, 128], f), "B8T": S_([128, 128], f), "B8": S_([128, 128], f),
     "D64": S_([128, 64], f), "D32": S_([128, 32], f), "MW": S_([128, 384], f),
     "LS": S_([128, 2048], b), "LW": S_([128, 2048], b), "CJ": S_([128, 192], b),
-    "RST": S_([128, 384], f), "RSB": S_([128, 3072], b), "EQ": S_([128, 12, 208], b),
-    "EQS": S_([128, 12, 208], b), "TRI": S_([128, 12, 16], b), "TIN": S_([128, 192], f),
-    "PMI": S_([128, 1], i4), "PMJ": S_([128, 1], i4), "PMF": S_([128, 1], f), "L16": S_([128, 12], f), "LN": S_([128, 12], f),
+    "RST": S_([128, 384], f), "RSB": S_([128, 3072], b), "EQ": S_([128, 1248], b), "MK": S_([128, 1248], b), "REV": S_([128, 128], f),
+    "UR": S_([128, 12], u2), "EL": S_([128, 2], u2), "PM2": S_([128, 1], f), "S1": S_([128, 1], f), "S2": S_([128, 1], f), "S3": S_([128, 1], f),
+    "EQS": S_([128, 1248], b), "TIN": S_([128, 16], f),
+    "PMI": S_([128, 1], i4), "PMJ": S_([128, 1], i4), "PMF": S_([128, 1], f), "L16": S_([128, 12], f), "LN": S_([128, 12], f), "LD": S_([128, 12], f), "PN": S_([128, 12], f),
     "KTI": S_([128, 12], i4), "KTF": S_([128, 12], f), "KT3": S_([128, 12], f), "E1C": S_([128, 12], f),
     "XD": S_([128, 12], f), "D4": S_([128, 48], f), "SL": S_([128, 3], f), "IOT": S_([128, V], f),
     "CC": S_([128, 96], i4), "U0": S_([128, 24], u2), "U1": S_([128, 24], u2), "U2": S_([128, 24], u2),
@@ -39,8 +42,8 @@ SCRATCH = {
     "PF": S_([128, 24], f), "F1": S_([128, 12], f), "FW": S_([128, 12], f),
     "QQ": S_([128, 4, 2, 12], f), "QD": S_([128, 48], f), "QP": S_([128, 48], f), "Q": S_([128, 48], f),
     "UAB": S_([128, 24], u2), "NE": S_([128, 12], f), "ME2": S_([128, 24], f), "UN": S_([128, 12], f), "THR": S_([128, 24], f),
-    "KL": S_([128, 384], u2), "KF": S_([128, 12, 2, 16], f), "KT": S_([128, 12, 32], f), "SD": S_([128, 384], f),
-    "XAB": S_([128, 384], b), "FR": S_([128, 192], u2), "CM": S_([128, 12], f), "CU": S_([128, 12], f), "CN": S_([128, 12], f),
+    "KL": S_([128, 384], u2), "KF": S_([128, 12, 2, 16], f), "SD": S_([128, 384], f),
+    "XAB": S_([128, 384], b), "FR": S_([128, 192], u2), "CM": S_([128, 16], f), "CU": S_([128, 12], f), "CN": S_([128, 12], f),
     "XA": S_([128, 3072], b), "XB": S_([128, 3072], b), "MA": S_([128, 192, 16], b), "MB": S_([128, 192, 16], b),
     "YA": S_([128, 3072], b), "YB": S_([128, 3072], b),
     "GA1": S_([128, 3072], b), "GB1": S_([128, 3072], b), "GA2": S_([128, 3072], b), "GB2": S_([128, 3072], b),
@@ -59,13 +62,13 @@ SCRATCH = {
 for _n in ("PXP", "PMX", "PKA", "PKB", "PD", "PC", "PH", "PS"):
     SCRATCH[_n] = ("psum", [128, 512], f)
 SMALL, _w = {}, 0
-for _n in ("PMF L16 LN KTF KT3 E1C XD SL T1 T2 PF F1 FW NE ME2 UN THR CM CU CN ZF ZD ZP NZ NZ2 M12 R12 WON BS B2 B3 "
+for _n in ("PMF L16 LD PN LN KTF KT3 E1C XD SL T1 T2 PF F1 FW NE ME2 UN THR CM CU CN ZF ZD ZP NZ NZ2 M12 R12 PM2 S1 S2 S3 WON BS B2 B3 "
            "OK1 OK2 DX DX2 SF WTF").split():
     SMALL[_n] = (_w, SCRATCH[_n][1][1])
     _w += (SCRATCH[_n][1][1] + 3) // 4 * 4
     del SCRATCH[_n]
 SCRATCH["SM"] = S_([128, _w], f)
-SCRATCH["PMX"] = ("psum", [128, 12, 32], f)
+SCRATCH["PMX"] = SCRATCH["PS"] = ("psum", [128, 12, 32], f)
 SEMAPHORES = ["v", "a", "p", "gq"] + ["arr%d" % t for t in range(RO)] + ["ls%d" % t for t in range(RO)] + \
     ["rl%d" % t for t in range(RO)] + ["rs"] + ["d%d" % k for k in range(20)] + ["g%d" % k for k in range(6)]
 
@@ -193,8 +196,12 @@ def rank_program(g, core, T, topo):
     def ms(x, c):
         do("v", lambda: g.vector.memset(x[0], c), x[1], [])
 
-    def act(out, in_):
-        do("a", lambda: g.scalar.activation(out[0], in_[0], AF.Copy), out[1], in_[1])
+    def act(out, in_, scale=1.0, bias=0.0):
+        rd = list(in_[1])
+        if not isinstance(scale, float):
+            rd += scale[1]
+            scale = scale[0]
+        do("a", lambda: g.scalar.activation(out[0], in_[0], AF.Copy, bias=bias, scale=scale), out[1], rd)
 
     def mm(out, l, r, st, sp):
         do("p", lambda: g.tensor.matmul(out[0], l[0], r[0], st, sp), out[1], l[1] + r[1])
@@ -246,39 +253,51 @@ def rank_program(g, core, T, topo):
     dma("s", T.PAI[0:8, 0:192], T.pa[:], [("PAI", 0, 192)], [])
     dma("s", T.PAI[0:8, 192:384], T.pb[:], [("PAI", 192, 384)], [])
     dma("a", T.WTI[:], T.wt[:], [("WTI", 0, 1)], [])
-    dma("gq", T.XW[:, 0:V], T.xs[:], [("XW", 0, V)], [])
-    dma("s", T.KDW[:, 0:V], T.kd[:], [("KDW", 0, V)], [])
 
     ms(o("ONE"), 1.0)
     ms(o("RST"), 1.0)
     ms(o("RST", 0, 384, 16), 0.0)
+    ms(o("LS"), 0.0)
     asel(o("MGT"), o("ONE"), [[1, 128]], OP.is_ge, 0, -16)
     asel(o("B8"), o("MGT"), [[-1, 128]], OP.is_ge, 15, 16)
     asel(o("IDF"), o("ONE"), [[-1, 128]], OP.is_equal, 0, 1)
     ts(o("DPF"), o("DPI"), 0.125, OP.mult)
     tt(o("FAC"), o("FAI"), o("DPF"), OP.add)
     dma("s", T.FAD[:], T.FAC[:], [("FAD", 0, V)], [("FAC", 0, 112)])
+    asel(o("MGT"), o("ONE"), [[-16, 8], [0, 16]], OP.is_ge, 0, 1)
+    asel(o("MG"), o("MGT"), [[16, 8], [0, 16]], OP.is_ge, 15, -1)
+    for k in range(8):
+        act(o("RSB", 384 * k, 384 * k + 384), o("RST"))
+    act(o("IDB"), o("IDF"))
+    act(o("NIB"), o("IDF"), -1.0)
+    for s in range(16):
+        act(o("LS", 128 * s + s, 128 * s + 128, 16), o("MG", 0, 128, 16), 16.0)
     for k in range(16):
         q = "s" if k % 2 == 0 else "a"
         dma(q, T.FAW[k:128:16, 0:V], T.FAD[:], [("FAW%d" % k, 0, V)], [("FAD", 0, V)], sem="d18" if q == "s" else "d19")
+    dma("s", T.KDW[:, 0:V], T.kd[:], [("KDW", 0, V)], [])
     acc["FAW"] = [(0, V, True, "d18", 128, "dma"), (0, V, True, "d19", 128, "dma")]
-    ms(o("RSB"), 1.0)
-    ms(o("RSB", 0, 3072, 16), 0.0)
+    ts(o("WTF"), o("WTI"), 1.0 / 16, OP.mult)
+    act(o("LW"), o("LS"), o("WTF"))
+    act(o("IHB"), o("IDF"), 0.5)
+    act(o("NIF"), o("IDF"), -1.0)
+    ms(o("XW", V, RT), 0.0)
     ms(o("PR0"), 0.0)
     ms(o("PR1"), 0.0)
     for k in range(4):
         ms(o("PR0", 32 * k, 32 * k + 16), 2.0 ** -12)
         ms(o("PR1", 32 * k + 16, 32 * k + 32), 2.0 ** -12)
-    asel(o("MGT"), o("ONE"), [[-16, 8], [0, 16]], OP.is_ge, 0, 1)
-    asel(o("MG"), o("MGT"), [[16, 8], [0, 16]], OP.is_ge, 15, -1)
     iota(o("PMI"), [[1, 1]], 0, 1)
     iota(o("L16"), [[16, 12]], 0, 0)
-    iota(o("TIN"), [[0, 12], [1, 16]], 0, 0)
+    iota(o("LD"), [[-16, 12]], 176, 0)
+    iota(o("TIN"), [[1, 16]], 0, 0)
+    asel(o("REV"), o("ONE"), [[-16, 8], [1, 16]], OP.is_equal, -15, 1)
     iota(o("CJ"), [[0, 12], [-1, 16]], 15, 0)
     asel(o("P00"), o("PR0"), [[-1, 128]], OP.is_equal, 0, 1)
     asel(o("P11"), o("PR1"), [[-1, 128]], OP.is_equal, 0, 1)
     asel(o("P01"), o("PR1"), [[-1, 128]], OP.is_equal, 16, 1)
     asel(o("P10"), o("PR0"), [[-1, 128]], OP.is_equal, -16, 1)
+    dma("gq", T.XW[:, 0:V], T.xs[:], [("XW", 0, V)], [])
     iota(o("IOT"), [[1, V]], 0, 0)
     send(0)
     tt(o("D64"), o("IDF", 0, 64), o("IDF", 64, 128), OP.add)
@@ -288,19 +307,18 @@ def rank_program(g, core, T, topo):
         cp(o("MW", a0, a0 + n), o("MW", 0, n))
     do("v", lambda: g.vector.tensor_copy(T.PAF[0:8, :], T.PAI[0:8, :]), [("PAF", 0, 384)], [("PAI", 0, 384)])
     do("p", lambda: g.tensor.matmul(T.PC[:, 0:384], T.B8[0:8, :], T.PAF[0:8, :], True, True), [("PC", 0, 384)], [("B8", 0, 128), ("PAF", 0, 384)])
-    tt(o("G"), o("PC", 0, 384), o("MW"), OP.mult)
-    scan(o("SD"), o("RST"), o("G"), OP.mult, OP.add)
-    cp(o("U0"), o("SD", 15, 384, 16))
-    cp(o("CC", 0, 24), o("SD", 15, 384, 16))
-    ms(o("LS"), 0.0)
-    ms(o("XW", V, RT), 0.0)
-    cp(o("IDB"), o("IDF"))
-    ts(o("NIB"), o("IDF"), -1.0, OP.mult)
     ts(o("PMJ"), o("PMI"), 15, OP.bitwise_and)
+    ms(o("MK"), 1.0)
     cp(o("PMF"), o("PMJ"))
-    for s in range(16):
-        ts(o("LS", 128 * s + s, 128 * s + 128, 16), o("MG", 0, 128, 16), 16.0, OP.mult)
-    ts(o("LN"), o("L16"), o("PMF"), OP.add)
+    tt(o("G"), o("PC", 0, 384), o("MW"), OP.mult)
+    ts(o("PM2"), o("PMF"), -1.0, OP.mult, 15.0, OP.add)
+    ts(o("PN"), o("L16"), o("PMF"), OP.add)
+    ts(o("LN"), o("LD"), o("PMF"), OP.add)
+    ts(o("MK", 0, 16), o("TIN"), o("PM2"), OP.is_gt)
+    scan(o("SD"), o("RST"), o("G"), OP.mult, OP.add)
+    for c in range(12):
+        cp((T.CC[:, c:13 + c:12], [("CC", c, c + 1), ("CC", c + 12, c + 13)]), o("SD", 191 - 16 * c, 384, 192))
+    do("v", lambda: g.vector.tensor_copy(T.U0[:], T.CC[:, 0:24]), [("U0", 0, 24)], [("CC", 0, 24)])
 
     fill = []
 
@@ -309,27 +327,28 @@ def rank_program(g, core, T, topo):
             fill.pop(0)()
 
     def twelfths(lst, ofs):
-        ts(o("N12", 0, 3), o("LN", 0, 3), 1.0 / 12, OP.mult, -11.0 / 24, OP.add)
+        ts(o("N12", 0, 3), o("PN", 0, 3), 1.0 / 12, OP.mult, -11.0 / 24, OP.add)
         ts(o("M12"), o("N12", 0, 3), -12.0, OP.mult, float(ofs), OP.add)
-        tt(o("R12"), o("LN", 0, 3), o("M12"), OP.add)
+        tt(o("R12"), o("PN", 0, 3), o("M12"), OP.add)
         cp(o(lst, 0, 3), o("R12"))
     fill += [
-        lambda: do("v", lambda: g.vector.tensor_scalar(T.TRI[:], T.TIN[:], o("PMF")[0], None, OP.is_lt), [("TRI", 0, 12)], [("TIN", 0, 192)] + o("PMF")[1]),
-        lambda: ts(o("WTF"), o("WTI"), 1.0 / 16, OP.mult),
-        lambda: ts(o("LW"), o("LS"), o("WTF"), OP.mult),
-        lambda: ts(o("IHB"), o("IDF"), 0.5, OP.mult),
-        lambda: ts(o("NIF"), o("IDF"), -1.0, OP.mult),
+        lambda: ts(o("S1"), o("PMF"), 1.0, OP.add),
+        lambda: ts(o("S2"), o("PMF"), -8.0, OP.mult, 192.0, OP.add),
+        lambda: tt(o("S3"), o("S1"), o("S2"), OP.mult),
+        lambda: ts(o("EL", 0, 1), o("S3"), -1.0, OP.add, 1247.0, OP.min),
         lambda: ts(o("KTI"), o("LN"), 1.0 / 3, OP.mult, -1.0 / 3, OP.add),
         lambda: ts(o("XD"), o("LN"), float(DO), OP.add),
         lambda: ts(o("KTF"), o("KTI"), -3.0, OP.mult),
-        lambda: ts(o("BS", 12, 24), o("LN"), float(UO), OP.add),
+        lambda: ts(o("BS", 12, 24), o("PN"), float(UO), OP.add),
         lambda: tt(o("KT3"), o("LN"), o("KTF"), OP.add),
-        lambda: ts(o("SL"), o("LN", 9, 12), 977.0, OP.mult),
+        lambda: ts(o("SL"), o("LN", 0, 3), 977.0, OP.mult),
         lambda: ts(o("E1C"), o("KT3"), 64.0, OP.mult, float(RT), OP.add),
         lambda: twelfths("LQ", 12),
         lambda: twelfths("LE", 24)]
+    for c in range(1, 12):
+        act(o("MK", 8 * c * (25 - c), 8 * c * (25 - c) + 16), o("MK", 0, 16))
     for k in range(4):
-        fill.append(lambda k=k: ts(o("D4", 12 * k, 12 * k + 12), o("LN"), float(V + 192 * (k % 2)), OP.add))
+        act(o("D4", 12 * k, 12 * k + 12), o("LN"), 1.0, float(V + 192 * (k % 2)))
 
     def r3(n, ap, lo, hi):
         return ap, [(n, lo, hi)]
@@ -367,78 +386,89 @@ def rank_program(g, core, T, topo):
         tt(o("H", 48, 72), o("H", 24, 48), o("H", 48, 72), OP.max)
         step(len(fill))
         tt(o("PRD"), o("DL"), o("H"), OP.mult)
+        tt(o("PF", 0, 12), o("H", 0, 12), o("DL", 24, 36), OP.mult)
         tt(o("T1"), o("PRD", 0, 24), o("PRD", 24, 48), OP.add)
         tt(o("T2"), o("PRD", 48, 72), o("CC", 72, 96), OP.add)
+        tt(o("PF", 12, 24), o("H", 24, 36), o("DL", 48, 60), OP.mult)
         do("v", lambda: g.vector.tensor_tensor(T.QQ[:, 0, :, :], o("T1")[0], o("T2")[0], OP.add), [("QQ", 0, 24)], o("T1")[1] + o("T2")[1])
+        tt(o("F1"), o("PF", 0, 12), o("PF", 12, 24), OP.add)
         do("v", lambda: g.vector.tensor_copy(T.UAB[:], T.QQ[:, 0, :, :]), [("UAB", 0, 24)], [("QQ", 0, 24)])
+        tt(o("NE"), qq(0, 0), qq(0, 1), OP.not_equal)
         cp(o("KL", 0, 192), ind("KDW", 0, V, "UAB", 0, 12))
         act(o("XAB"), ind("XW", 0, V, "UAB", 0, 24))
+        mm(o("PD", 0, 12), o("REV"), qq(0, 0), True, True)
         mm(o("PXP", 0, 384), o("IDB"), o("XAB"), True, True)
         for hf in range(2):
-            act(o("XA", 1536 * hf, 1536 * hf + 1536), ind("XW", 0, V, "KL", 96 * hf, 96 * hf + 96))
+            l0, l1 = PARTS[hf]
+            act(o("XA", 16 * l0, 16 * l1), ind("XW", 0, V, "KL", l0, l1))
         cp(o("KL", 192, 384), ind("KDW", 0, V, "UAB", 12, 24))
         for hf in range(2):
-            act(o("XB", 1536 * hf, 1536 * hf + 1536), ind("XW", 0, V, "KL", 192 + 96 * hf, 288 + 96 * hf))
+            l0, l1 = PARTS[hf]
+            act(o("XB", 16 * l0, 16 * l1), ind("XW", 0, V, "KL", 192 + l0, 192 + l1))
         cp(r3("KF", T.KF[:], 0, 12), o("KL"))
         for gp in range(2):
             for cq in range(2):
                 mm((T.PMX[:, :, 16 * gp:16 * gp + 16], [("PMX", 0, 12)]), o("P%d%d" % (gp, cq)), (T.KF[:, :, cq, :], [("KF", 0, 12)]), cq == 0, cq == 1)
-        tt(o("PF", 0, 12), o("H", 0, 12), o("DL", 24, 36), OP.mult)
-        tt(o("PF", 12, 24), o("H", 24, 36), o("DL", 48, 60), OP.mult)
-        tt(o("F1"), o("PF", 0, 12), o("PF", 12, 24), OP.add)
         tt(o("FW"), o("F1"), o("CC", 72, 84), OP.add)
-        tt(o("NE"), qq(0, 0), qq(0, 1), OP.not_equal)
         tt(o("ME2", 0, 12), o("NE"), o("H", 48, 60), OP.mult)
-        tt(o("ME2", 12, 24), o("NE"), o("H", 48, 60), OP.mult)
-        ts(o("UN"), o("ME2", 0, 12), -1.0, OP.mult, 1.0, OP.add)
-        ts(o("THR"), o("ME2"), -4096.0, OP.mult, 4096.0 + 143.0, OP.add)
-        cp(o("FR"), ind("FAW", 0, V, "UAB", 0, 12))
-        for c in range(12):
-            ts(r3("EQ", T.EQ[:, c, 192 - 16 * c:208], c, c + 1), o("FR", 0, 16 * c + 16), o("FW", c, c + 1), OP.is_equal)
+        cp(o("UR"), o("PD", 0, 12))
+        cp(o("FR"), ind("FAW", 0, V, "UR", 0, 12))
+
+        def equal_f(c):
+            e0 = 8 * c * (25 - c)
+            ts(o("EQ", e0, e0 + 192 - 16 * c), o("FR", 16 * c, 192), o("FW", c, c + 1), OP.is_equal)
+        for c in range(NEQ):
+            equal_f(c)
         for sd in range(2):
             xn, mn, gn, pk = ("XA", "XB")[sd], ("MA", "MB")[sd], ("GA1", "GB1")[sd], ("PKA", "PKB")[sd]
             for hf in range(2):
-                l0, l1 = 96 * hf, 96 * hf + 96
+                l0, l1 = PARTS[hf]
                 for j in range(0 if sd and hf in PE_HALVES else 16):
                     tt(r3("%s_%d" % (mn, j), T[mn][:, l0:l1, j], l0, l1), o(xn, 16 * l0 + j, 16 * l1, 16), o("PXP", 192 * (1 - sd) + l0, 192 * (1 - sd) + l1), OP.max)
-                mm(o(pk, 96 * hf, 96 * hf + 96), o("IDB"), o("CJ", 0, 96), True, False)
+                mm(o(pk, l0, l1), o("IDB"), o("CJ", l0, l1), True, False)
                 for s in range(16):
-                    mm(o(pk, 96 * hf, 96 * hf + 96), o("LS", 128 * s, 128 * s + 128), (T[mn][:, l0 + s:l1:16, :], [("%s_%d" % (mn, j), l0, l1) for j in range(16)]), False, s == 15)
+                    mm(o(pk, l0, l1), o("LS", 128 * s, 128 * s + 128), (T[mn][:, l0 + s:l1:16, :], [("%s_%d" % (mn, j), l0, l1) for j in range(16)]), False, s == 15)
                 scan(o(gn, 16 * l0, 16 * l1), o("RSB", 16 * l0, 16 * l1), o(xn, 16 * l0, 16 * l1), OP.mult, OP.max)
             for hf in (() if sd else PE_HALVES):
-                l0, l1 = 96 * hf, 96 * hf + 96
+                l0, l1 = PARTS[hf]
                 for j4 in range(4):
-                    pb = ("PD", "PC", "PH", "PS")[j4]
+                    pb = ("PC", "PH", "PD")[j4 % 3]
                     for j in range(4):
-                        po = o(pb, j, 384, 4)
+                        po = o(pb, j, 4 * (l1 - l0), 4)
                         mm(po, o("IDB"), o("XB", 16 * l0 + 4 * j4 + j, 16 * l1, 16), True, False)
                         mm(po, o("NIB"), o("XAB", l0, l1), False, True)
-                    do("a", lambda: g.scalar.activation(T.MB[:, l0:l1, 4 * j4:4 * j4 + 4], T[pb][:, 0:384], AF.Relu),
-                       [("MB_%d" % (4 * j4 + j), l0, l1) for j in range(4)], [(pb, 0, 384)])
+                    do("a", lambda: g.scalar.activation(T.MB[:, l0:l1, 4 * j4:4 * j4 + 4], T[pb][:, 0:4 * (l1 - l0)], AF.Relu),
+                       [("MB_%d" % (4 * j4 + j), l0, l1) for j in range(4)], [(pb, 0, 512)])
             if sd == 0:
-                do("v", lambda: g.vector.transpose(T.KT[:], T.PMX[:]), [("KT", 0, 12)], [("PMX", 0, 12)])
-                if not last:
-                    tt(o("G"), ind("KDW", 0, V, "UAB", 0, 24), o("MW"), OP.mult)
+                do("v", lambda: g.vector.transpose(T.PS[:], T.PMX[:]), [("PS", 0, 12)], [("PMX", 0, 12)])
+                fill += [lambda c=c: equal_f(c) for c in range(NEQ, 12)]
+                step(len(fill) - 5)
             else:
-                eqb = r3("EQ", T.EQ[:, :, 192:208], 0, 12)
-                tt(eqb, eqb, r3("TRI", T.TRI[:], 0, 12), OP.mult)
+                scan(o("EQS"), o("EQ"), o("MK"), OP.max, OP.mult)
                 if not last:
+                    tt(o("G"), o("MW"), r3("PS", T.PS[:], 0, 12), OP.mult)
                     scan(o("SD"), o("RST"), o("G"), OP.mult, OP.add)
-                for c in range(12):
-                    e = r3("EQ", T.EQ[:, c, 192 - 16 * c:208], c, c + 1)
-                    scan(r3("EQS", T.EQS[:, c, 192 - 16 * c:208], c, c + 1), e, e, OP.max, OP.max)
-                if not last:
-                    act(qq(2), o("SD", 15, 384, 16))
-                ts(o("CM"), r3("EQS", T.EQS[:, :, 207], 0, 12), -1.0, OP.mult, 1.0, OP.add)
+                fill += [lambda: ts(o("CM"), ind("EQS", 0, 1248, "EL", 0, 1), -1.0, OP.mult, 1.0, OP.add),
+                         lambda: tt(o("CU"), o("CM", 0, 12), o("UN"), OP.mult)]
             scan(o("RUN"), o("RST", 0, 192), o(pk, 0, 192), OP.mult, OP.max)
+            step()
             tt(o("TT"), o("RUN"), o(pk, 0, 192), OP.subtract)
-            tt(o("DD"), r3("KT", T.KT[:, 6 * sd:6 * sd + 6, :], 6 * sd, 6 * sd + 6), o("TT"), OP.subtract)
+            step()
+            tt(o("DD"), r3("PS", T.PS[:, 6 * sd:6 * sd + 6, :], 6 * sd, 6 * sd + 6), o("TT"), OP.subtract)
+            step()
             scan(o("LSC"), o("TT"), o("DD"), OP.min, OP.max)
+            step()
             le = o("LSC", 15, 192, 16)
             ts(o("UL3", 12 * sd, 12 * sd + 12), le, 4096.0, OP.mult)
+            step()
             cp(o("K2", 192 * sd, 192 * sd + 192), ind("KDW", 0, V, "UL3", 12 * sd, 12 * sd + 12))
-            ts(qq(1, sd), le, 4096.0, OP.mult)
+            act(qq(1, sd), le, 4096.0)
             if sd == 0:
+                act(o("ME2", 12, 24), o("ME2", 0, 12))
+                act(o("UN"), o("ME2", 0, 12), -1.0, 1.0)
+                act(o("THR", 0, 12), o("ME2", 0, 12), -4096.0, 4096.0 + 143.0)
+                act(o("THR", 12, 24), o("ME2", 0, 12), -4096.0, 4096.0 + 143.0)
+                act(o("B2", 0, 12), o("E1C"), 1.0, float(192 * rnd))
                 ts(o("UL3", 24, 36), le, 4096.0, OP.mult)
             k2 = 192 * sd
             act(o(("YA", "YB")[sd], 0, 1536), ind("XW", 0, V, "K2", k2, k2 + 96))
@@ -448,15 +478,15 @@ def rank_program(g, core, T, topo):
                 act(o("YB", 1536, 16 * VL), ind("XW", 0, V, "K2", 288, 192 + VL))
                 if VL < 192:
                     cp(o("YB", 16 * VL, 3072), ind("XW", 0, V, "K2", 192 + VL, 384))
-                tt(o("CU"), o("CM"), o("UN"), OP.mult)
                 if not last:
+                    act(qq(2), o("SD", 15, 384, 16), 4096.0)
                     act(o("LR"), ind("IOT", 0, V, "UL3", 0, 24))
                 act(o("FV"), ind("FAW", 0, V, "UL3", 12, 36))
         for s in range(16):
             kw = o("LW", 128 * s, 128 * s + 128)
             mm(o("PH", 0, 12), kw, o("GA1", 16 * s + 15, 3072, 256), s == 0, False)
             if not last:
-                mm(o("PS", 0, 3), kw, o("GB1", 2304 + 16 * s + 15, 3072, 256), s == 0, False)
+                mm(r3("PS", T.PS[:, 0, 0:3], 0, 12), kw, o("GB1", 16 * s + 15, 768, 256), s == 0, False)
         lf = qq(1)
         ts(o("ZF"), lf, float(Z), OP.is_equal)
         tt(o("ZD"), qq(0), lf, OP.subtract)
@@ -464,11 +494,8 @@ def rank_program(g, core, T, topo):
         tt(o("ZP"), o("ZD"), o("ZF"), OP.mult)
         ts(o("NZ2"), o("NZ"), -1.0, OP.mult, 1.0, OP.add)
         tt(qq(3), lf, o("ZP"), OP.add)
-        tt(o("CN"), o("CM"), o("NZ2"), OP.mult)
         if last:
             cp(qq(2), qq(1))
-        do("v", lambda: g.vector.tensor_tensor(T.QD[:], T.QQ[:, :, 1, :], T.QQ[:, :, 0, :], OP.subtract), [("QD", 0, 48)], [("QQ", 0, 96)])
-        do("v", lambda: g.vector.tensor_tensor(T.E4[:], T.QQ[:, 0:2, :, :], T.D4[:], OP.subtract), [("E4", 0, 48)], [("QQ", 0, 48), ("D4", 0, 48)])
         for sd in range(2):
             xn, gn = ("YA", "YB")[sd], ("GA2", "GB2")[sd]
             for hf in range(2):
@@ -488,23 +515,25 @@ def rank_program(g, core, T, topo):
         mm(o("PD", 0, 192), o("NIB"), o("GB2", 15, 3072, 16), False, True)
         if not last:
             for s in range(16):
-                mm(o("PS", 0, 3), o("LW", 128 * s, 128 * s + 128), o("GB2", 2304 + 16 * s + 15, 3072, 256), False, s == 15)
+                mm(r3("PS", T.PS[:, 0, 0:3], 0, 12), o("LW", 128 * s, 128 * s + 128), o("GB2", 16 * s + 15, 768, 256), False, s == 15)
         ts(o("CMP", 0, 192), o("PD", 0, 192), 0.0, OP.is_gt)
         ts(o("CMP", 192, 384), o("PD", 0, 192), 0.0, OP.is_lt)
         for s in range(16):
             mm(o("PC", 0, 24), o("LS", 128 * s, 128 * s + 128), o("CMP", s, 384, 16), s == 0, s == 15)
+        do("v", lambda: g.vector.tensor_tensor(T.QD[:], T.QQ[:, :, 1, :], T.QQ[:, :, 0, :], OP.subtract), [("QD", 0, 48)], [("QQ", 0, 96)])
+        do("v", lambda: g.vector.tensor_tensor(T.E4[:], T.QQ[:, 0:2, :, :], T.D4[:], OP.subtract), [("E4", 0, 48)], [("QQ", 0, 48), ("D4", 0, 48)])
+        tt(o("CN"), o("CM", 0, 12), o("NZ2"), OP.mult)
         cp(o("HI"), o("PH", 0, 12))
-        ts(o("B2", 0, 12), o("E1C"), float(192 * rnd), OP.add)
         ts(o("HJ"), o("HI"), 63, OP.bitwise_and)
         if not last:
-            tt(o("SH"), o("HI", 9, 12), o("SL"), OP.add)
+            tt(o("SH"), o("HI", 0, 3), o("SL"), OP.add)
         tt(o("BS", 0, 12), o("B2", 0, 12), o("HJ"), OP.add)
         tt(o("WB", 0, 24), o("PC", 0, 24), o("THR"), OP.is_ge)
         xe = RT + 192 * rnd + 192
 
         def new_x(xe=xe, last=last):
             return [
-                lambda: tt(o("OK1"), o("CM"), o("WON"), OP.mult),
+                lambda: tt(o("OK1"), o("CM", 0, 12), o("WON"), OP.mult),
                 lambda: tt(o("DX"), o("Q", 0, 12), o("XD"), OP.subtract),
                 lambda: tt(o("OK2"), o("OK1"), o("CU"), OP.add),
                 lambda: tt(o("XS"), ind("XW", 0, xe, "EU", 0, 12), o("XE"), OP.add),
@@ -520,13 +549,14 @@ def rank_program(g, core, T, topo):
                 tt(o("NK", 32 * h0, 32 * h0 + 192), r3("KF", T.KF[:, h0:h0 + 6, :, :], h0, h0 + 6), o("MM", 32 * h0, 32 * h0 + 192),
                    OP.subtract if h0 else OP.add)
             return [
-                lambda: tt(o("OH"), r3("KF", T.KF[:], 0, 12), o("LR"), OP.is_equal),
+                lambda: tt(o("OH"), r3("KF", T.KF[:], 0, 12), o("PKB", 0, 384), OP.is_equal),
                 lambda: tt(o("MM", 0, 192), o("OH", 0, 192), o("PKA", 0, 192), OP.mult),
                 lambda: tt(o("MM", 192, 384), o("OH", 192, 384), o("PKA", 0, 192), OP.mult),
                 lambda: half(0),
                 lambda: half(6)]
 
         if not last:
+            mm(o("PKB", 0, 384), o("IDF"), o("LR"), True, True)
             mm(o("PKA", 0, 192), o("IDF"), o("LR", 192, 384), True, False)
             mm(o("PKA", 0, 192), o("NIF"), o("LR", 0, 192), False, True)
         tt(o("WON"), o("WB", 0, 12), o("WB", 12, 24), OP.add)
@@ -538,7 +568,7 @@ def rank_program(g, core, T, topo):
         tt(o("DS"), o("D4"), o("EP"), OP.add)
         tt(o("B3"), o("B2"), o("ME2"), OP.mult)
         if not last:
-            tt(o("SI"), o("PS", 0, 3), o("SH"), OP.add)
+            tt(o("SI"), r3("PS", T.PS[:, 0, 0:3], 0, 12), o("SH"), OP.add)
         cp(o("DU"), o("DS"))
         tt(o("B2"), o("BS"), o("B3"), OP.add)
         if not last:
@@ -546,21 +576,18 @@ def rank_program(g, core, T, topo):
         cp(o("EU"), o("B2"))
         act(o("XE"), ind("XW", 0, xe, "EU", 12, 24))
         if last:
-            ops = new_x()
-            for p in ops[:3]:
-                p()
-            cp(scat("FAW", 0, 2176, "DU", 24, 48), o("FV"))
-            dma("s", T.YFA[:], T.FAW[0:128:16, 0:V], [("YFA", 0, 112)], [("FAW", 0, V)])
-            for p in ops[3:]:
+            for p in new_x():
                 p()
             dma("gq", T.yx[:], T.XW[:, 0:V], [("yx", 0, V)], [("XW", 0, V)])
+            cp(scat("FAW", 0, 2176, "DU", 24, 48), o("FV"))
+            dma("s", T.YFA[:], T.FAW[0:128:16, 0:V], [("YFA", 0, 112)], [("FAW", 0, V)])
             tt(o("YFB"), o("YFA"), o("DPF"), OP.subtract)
             dma("s", T.yf[:], T.YFB[:], [("yf", 0, V)], [("YFB", 0, 112)])
             break
         cp(o("CC", 0, 12), o("Q", 36, 48))
         ts(o("SF"), o("SJ"), float(V), OP.is_ge, float(V), OP.mult)
-        cp(o("CC", 12, 21), o("Q", 24, 33))
-        tt(o("CC", 21, 24), o("SJ"), o("SF"), OP.subtract)
+        cp(o("CC", 15, 24), o("Q", 27, 36))
+        tt(o("CC", 12, 15), o("SJ"), o("SF"), OP.subtract)
         cp(scat("FAW", 0, 2176, "DU", 24, 48), o("FV"))
         cp(o("U0"), o("CC", 0, 24))
         fill += new_k() + new_x() + [lambda rnd=rnd: send(rnd + 1)]

from concourse.bass import DstId, RemoteDMATransfer
from concourse.mybir import AluOpType as OP, ActivationFunctionType as AF

V, R, LA, RO, Z = 1792, 64, 192, 4, 1791
UO, DO, RT = 1792, 1984, 2176
XC = RT + 192 * RO
f, b, i4, u2 = "float32", "bfloat16", "int32", "uint16"


VL = 128
NEQ = 4
PARTS = ((0, 96), (96, 192))
PE_HALVES = (0,)


def S_(shape, d):
    return ("sbuf", shape, d)


SCRATCH = {
    "XW": S_([128, XC], f), "KDW": S_([128, 2176], i4), "FAW": S_([128, 2176], f),
    "FAD": ("dram", [8, V], f), "FAI": S_([128, 112], i4), "DPI": S_([128, 112], i4), "DPF": S_([128, 112], f),
    "FAC": S_([128, 112], f), "YFA": S_([128, 112], f), "YFB": S_([128, 112], f),
    "PAI": S_([128, 384], i4), "PAF": S_([128, 384], f), "WTI": S_([128, 1], i4), "WTF": S_([128, 1], f),
    "ONE": S_([128, 128], f), "IDF": S_([128, 128], f), "NIF": S_([128, 128], f),
    "IDB": S_([128, 128], b), "NIB": S_([128, 128], b), "IHB": S_([128, 128], b),
    "PR0": S_([128, 128], f), "PR1": S_([128, 128], f),
    "P00": S_([128, 128], f), "P11": S_([128, 128], f), "P01": S_([128, 128], f), "P10": S_([128, 128], f),
    "MGT": S_([128, 128], f), "MG": S_([128, 128], f), "B8T": S_([128, 128], f), "B8": S_([128, 128], f),
    "D64": S_([128, 64], f), "D32": S_([128, 32], f), "MW": S_([128, 384], f),
    "LS": S_([128, 2048], b), "LW": S_([128, 2048], b), "CJ": S_([128, 192], b),
    "RST": S_([128, 384], f), "RSB": S_([128, 3072], b), "EQ": S_([128, 1248], b), "MK": S_([128, 1248], b), "REV": S_([128, 128], f),
    "UR": S_([128, 12], u2), "EL": S_([128, 2], u2), "PM2": S_([128, 1], f), "S1": S_([128, 1], f), "S2": S_([128, 1], f), "S3": S_([128, 1], f),
    "EQS": S_([128, 1248], b), "TIN": S_([128, 16], f),
    "PMI": S_([128, 1], i4), "PMJ": S_([128, 1], i4), "PMF": S_([128, 1], f), "L16": S_([128, 12], f), "LN": S_([128, 12], f), "LD": S_([128, 12], f), "PN": S_([128, 12], f),
    "KTI": S_([128, 12], i4), "KTF": S_([128, 12], f), "KT3": S_([128, 12], f), "E1C": S_([128, 12], f),
    "XD": S_([128, 12], f), "D4": S_([128, 48], f), "SL": S_([128, 3], f), "IOT": S_([128, V], f),
    "CC": S_([128, 96], i4), "U0": S_([128, 24], u2), "U1": S_([128, 24], u2), "U2": S_([128, 24], u2),
    "G": S_([128, 384], f), "SB": S_([128, 1152], f), "Y": S_([128, 5, 36], f),
    "E0": S_([128, 3, 24], f), "E1": S_([128, 3, 24], f), "E2": S_([128, 3, 24], f), "H": S_([128, 72], f),
    "DL": S_([128, 72], f), "PRD": S_([128, 72], f), "T1": S_([128, 24], f), "T2": S_([128, 24], f),
    "PF": S_([128, 24], f), "F1": S_([128, 12], f), "FW": S_([128, 12], f),
    "QQ": S_([128, 4, 2, 12], f), "QD": S_([128, 48], f), "QP": S_([128, 48], f), "Q": S_([128, 48], f),
    "UAB": S_([128, 24], u2), "NE": S_([128, 12], f), "ME2": S_([128, 24], f), "UN": S_([128, 12], f), "THR": S_([128, 24], f),
    "KL": S_([128, 384], u2), "KF": S_([128, 12, 2, 16], f), "SD": S_([128, 384], f),
    "XAB": S_([128, 384], b), "FR": S_([128, 192], u2), "CM": S_([128, 16], f), "CU": S_([128, 12], f), "CN": S_([128, 12], f),
    "XA": S_([128, 3072], b), "XB": S_([128, 3072], b), "MA": S_([128, 192, 16], b), "MB": S_([128, 192, 16], b),
    "YA": S_([128, 3072], b), "YB": S_([128, 3072], b),
    "GA1": S_([128, 3072], b), "GB1": S_([128, 3072], b), "GA2": S_([128, 3072], b), "GB2": S_([128, 3072], b),
    "RUN": S_([128, 192], f), "TT": S_([128, 192], f), "DD": S_([128, 192], f), "LSC": S_([128, 192], f),
    "UL3": S_([128, 36], u2), "K2": S_([128, 384], u2), "ZF": S_([128, 24], f), "ZD": S_([128, 24], f), "ZP": S_([128, 24], f),
    "NZ": S_([128, 12], f), "NZ2": S_([128, 12], f), "LR": S_([128, 384], f), "OH": S_([128, 384], f), "MM": S_([128, 384], f),
    "NK": S_([128, 384], i4), "FV": S_([128, 384], f), "CMP": S_([128, 384], b), "WON": S_([128, 12], f),
    "E4": S_([128, 48], f), "EP": S_([128, 48], f), "DS": S_([128, 48], f), "DU": S_([128, 48], u2),
    "HI": S_([128, 12], i4), "HJ": S_([128, 12], i4), "BS": S_([128, 24], f), "B2": S_([128, 24], f), "B3": S_([128, 24], f),
    "EU": S_([128, 24], u2), "OK1": S_([128, 12], f), "OK2": S_([128, 12], f), "DX": S_([128, 12], f), "DX2": S_([128, 12], f),
    "XU": S_([128, 12], u2), "XE": S_([128, 192], f), "XS": S_([128, 192], f), "XN": S_([128, 192], i4),
    "SI": S_([128, 3], i4), "SJ": S_([128, 3], i4), "SF": S_([128, 3], f), "SH": S_([128, 3], f),
    "RB": S_([128, 64 * RO], f), "N12": S_([128, 4], i4), "M12": S_([128, 3], f), "R12": S_([128, 3], f),
    "LQ": S_([128, 4], u2), "LE": S_([128, 4], u2), "WB": S_([128, 40], f),
}
for _n in ("PXP", "PMX", "PKA", "PKB", "PD", "PC", "PH", "PS"):
    SCRATCH[_n] = ("psum", [128, 512], f)
SMALL, _w = {}, 0
for _n in ("PMF L16 LD PN LN KTF KT3 E1C XD SL T1 T2 PF F1 FW NE ME2 UN THR CM CU CN ZF ZD ZP NZ NZ2 M12 R12 PM2 S1 S2 S3 WON BS B2 B3 "
           "OK1 OK2 DX DX2 SF WTF").split():
    SMALL[_n] = (_w, SCRATCH[_n][1][1])
    _w += (SCRATCH[_n][1][1] + 3) // 4 * 4
    del SCRATCH[_n]
SCRATCH["SM"] = S_([128, _w], f)
SCRATCH["PMX"] = SCRATCH["PS"] = ("psum", [128, 12, 32], f)
SEMAPHORES = ["v", "a", "p", "gq"] + ["arr%d" % t for t in range(RO)] + ["ls%d" % t for t in range(RO)] + \
    ["rl%d" % t for t in range(RO)] + ["rs"] + ["d%d" % k for k in range(20)] + ["g%d" % k for k in range(6)]


def relay_of(core, dst, topo):
    c = [x for x in topo.cores_of(core) if x != core and topo.may_write(x, dst)]
    return sorted(c, key=lambda x: (topo.die(x) != topo.die(core), x))[0]


def split(core, topo, T):
    near = [d for d in T.cores if d != core and topo.may_write(core, d)]
    far = [d for d in T.cores if d != core and not topo.may_write(core, d)]
    return near, far, (relay_of(core, far[0], topo) if far else None)


def land(T, src, dst, t):
    k = (T.rank_of(src) - T.rank_of(dst) - 1) % len(T.cores)
    return RT + 192 * t + 64 * k


def did(d, src, topo):
    rid, pid = topo.addr(d, src)
    return DstId(rid=rid, pnc=pid)


def bits(es):
    return sum(1 << e for e in es)


def relay_program(g, core, T, topo, src):
    far = split(src, topo, T)[1]
    es = [topo.engines(core, d) for d in far]
    n = 0
    for t in range(RO):
        g.wait_ge(T.sem["rl%d" % t], 4)
        tr = []
        for k, d in enumerate(far):
            c = land(T, src, d, t)
            tr.append(RemoteDMATransfer(dst_ids=[did(d, core, topo)], dma_engine_mask=bits(es[k][4 * k:4 * k + 4]),
                                        remote_sem=T.sem["arr%d" % t], srcs=[T.RB[:, 64 * t:64 * t + 64]], dsts=[T.XW[:, c:c + 64]]))
            n += 4
        g.remote_dma_fused(tr, local_sem=T.sem.rs)
    g.wait_ge(T.sem.rs, n)


def rank_program(g, core, T, topo):
    if T.rank_of(core) is None:
        for src in T.cores:
            if split(src, topo, T)[2] == core:
                relay_program(g, core, T, topo, src)
        return
    eng = {"v": g.vector, "a": g.scalar, "p": g.tensor, "gq": g, "s": g.sync}
    acc, total, waited, snap = {}, {}, {}, {}
    know = {q: {} for q in eng}

    def do(q, call, W, Rd, sem=None, inc=1):
        dma = sem is not None
        me = "dma" if dma else q
        need = {}

        def want(e):
            need[e[3]] = max(need.get(e[3], 0), e[4])
        for n, lo, hi in Rd:
            for e in acc.get(n, []):
                if (e[0] < hi and lo < e[1] and e[2]) or (n in PS and e[5] != me):
                    want(e)
        for n, lo, hi in W:
            for e in acc.get(n, []):
                if (n in PS and e[5] != me) or (e[0] < hi and lo < e[1] and not (me == "p" and e[5] == "p")):
                    want(e)
        for s, val in need.items():
            val = total.get(s, val) if s[0] in "d" or (s[0] == "g" and s != "gq") else val
            if know[q].get(s, 0) < val:
                eng[q].wait_ge(T.sem[s], val)
                waited[s] = max(waited.get(s, 0), val)
                for k, x in snap.get((s, val), {}).items():
                    know[q][k] = max(know[q].get(k, 0), x)
                know[q][s] = val
        r = call()
        s = sem if dma else q
        r.then_inc(T.sem[s], inc)
        total[s] = total.get(s, 0) + inc
        snap[(s, total[s])] = dict(know[q])
        for n, lo, hi in W:
            acc[n] = [e for e in acc.get(n, []) if not (lo <= e[0] and e[1] <= hi)]
            acc[n].append((lo, hi, True, s, total[s], me))
        for n, lo, hi in Rd:
            acc[n] = [e for e in acc.get(n, []) if not (not e[2] and e[0] == lo and e[1] == hi and e[5] == me and me != "dma")]
            acc[n].append((lo, hi, False, s, total[s], me))

    PS = ("PXP", "PMX", "PKA", "PKB", "PD", "PC", "PH", "PS")

    def o(n, lo=0, hi=None, st=1):
        if n in SMALL:
            w0, w = SMALL[n]
            n, lo, hi = "SM", w0 + lo, w0 + (w if hi is None else hi)
        hi = T[n].shape[1] if hi is None else hi
        return (T[n][:, lo:hi] if st == 1 else T[n][:, lo:hi:st]), [(n, lo, hi)]

    def ind(n, lo, hi, on, oc, od):
        return T[n][:, lo:hi].indirect(T[on][:, oc:od]), [(n, lo, hi), (on, oc, od)]

    def scat(n, lo, hi, on, oc, od):
        return T[n][:, lo:hi].indirect(T[on][:, oc:od]), [(n, lo, hi)], [(on, oc, od)]

    def cp(out, in_):
        do("v", lambda: g.vector.tensor_copy(out[0], in_[0]), out[1], in_[1] + (out[2] if len(out) > 2 else []))

    def tt(out, x, y, op):
        do("v", lambda: g.vector.tensor_tensor(out[0], x[0], y[0], op), out[1], x[1] + y[1])

    def ts(out, x, s1, op0, s2=None, op1=None):
        rd = list(x[1])
        if not isinstance(s1, (int, float)):
            rd += s1[1]
            s1 = s1[0]
        if op1 is None:
            do("v", lambda: g.vector.tensor_scalar(out[0], x[0], s1, None, op0), out[1], rd)
        else:
            do("v", lambda: g.vector.tensor_scalar(out[0], x[0], s1, s2, op0, op1), out[1], rd)

    def scan(out, d0, d1, op0, op1):
        do("v", lambda: g.vector.tensor_tensor_scan(out[0], d0[0], d1[0], 0.0, op0, op1), out[1], d0[1] + d1[1])

    def ms(x, c):
        do("v", lambda: g.vector.memset(x[0], c), x[1], [])

    def act(out, in_, scale=1.0, bias=0.0):
        rd = list(in_[1])
        if not isinstance(scale, float):
            rd += scale[1]
            scale = scale[0]
        do("a", lambda: g.scalar.activation(out[0], in_[0], AF.Copy, bias=bias, scale=scale), out[1], rd)

    def mm(out, l, r, st, sp):
        do("p", lambda: g.tensor.matmul(out[0], l[0], r[0], st, sp), out[1], l[1] + r[1])

    def iota(x, pat, base, cm):
        do("gq", lambda: g.iota(x[0], pat, base, cm, allow_small_or_imprecise_dtypes=True), x[1], [])

    def asel(out, x, pat, op, base, cm):
        do("gq", lambda: g.affine_select(out[0], x[0], pat, op, 0.0, base, cm), out[1], x[1])

    nd = [0, 0]

    def dma(q, out, in_, W, Rd, sem=None):
        if sem is None:
            sem = ("g%d" % nd[1]) if q == "gq" else ("d%d" % nd[0])
            nd[1 if q == "gq" else 0] += 1
        do(q, lambda: eng[q].dma_start(out, in_), W, Rd, sem, 16)
        return sem

    for t in range(RO):
        acc.setdefault("XW", []).append((RT + 192 * t, RT + 192 * t + 192, True, "arr%d" % t, 12, "dma"))
        total["arr%d" % t] = 12

    near, far, rel = split(core, topo, T)
    en = topo.engines(core, near[0])[:4]
    er = [e for e in topo.engines(core, rel) if e not in en][:4]

    def send(t):
        need = {}
        for e in acc["XW"]:
            if e[2] and e[0] < 64:
                need[e[3]] = max(need.get(e[3], 0), e[4])
        for s, val in need.items():
            if know["gq"].get(s, 0) < val:
                g.wait_ge(T.sem[s], val)
                waited[s] = max(waited.get(s, 0), val)
                know["gq"][s] = val
        c = land(T, core, near[0], t)
        g.remote_dma_fused([
            RemoteDMATransfer(dst_ids=[did(near[0], core, topo)], dma_engine_mask=bits(en), remote_sem=T.sem["arr%d" % t],
                              srcs=[T.XW[:, 0:64]], dsts=[T.XW[:, c:c + 64]]),
            RemoteDMATransfer(dst_ids=[did(rel, core, topo)], dma_engine_mask=bits(er), remote_sem=T.sem["rl%d" % t],
                              srcs=[T.XW[:, 0:64]], dsts=[T.RB[:, 64 * t:64 * t + 64]])], local_sem=T.sem["ls%d" % t])
        total["ls%d" % t] = 8
        acc["XW"].append((0, 64, False, "ls%d" % t, 8, "dma"))

    dma("s", T.FAI[:], T.fa[:], [("FAI", 0, 112)], [])
    dma("a", T.DPI[:], T.dp[:], [("DPI", 0, 112)], [])
    dma("s", T.PAI[0:8, 0:192], T.pa[:], [("PAI", 0, 192)], [])
    dma("s", T.PAI[0:8, 192:384], T.pb[:], [("PAI", 192, 384)], [])
    dma("a", T.WTI[:], T.wt[:], [("WTI", 0, 1)], [])

    ms(o("ONE"), 1.0)
    ms(o("RST"), 1.0)
    ms(o("RST", 0, 384, 16), 0.0)
    ms(o("LS"), 0.0)
    asel(o("MGT"), o("ONE"), [[1, 128]], OP.is_ge, 0, -16)
    asel(o("B8"), o("MGT"), [[-1, 128]], OP.is_ge, 15, 16)
    asel(o("IDF"), o("ONE"), [[-1, 128]], OP.is_equal, 0, 1)
    ts(o("DPF"), o("DPI"), 0.125, OP.mult)
    tt(o("FAC"), o("FAI"), o("DPF"), OP.add)
    dma("s", T.FAD[:], T.FAC[:], [("FAD", 0, V)], [("FAC", 0, 112)])
    asel(o("MGT"), o("ONE"), [[-16, 8], [0, 16]], OP.is_ge, 0, 1)
    asel(o("MG"), o("MGT"), [[16, 8], [0, 16]], OP.is_ge, 15, -1)
    for k in range(8):
        act(o("RSB", 384 * k, 384 * k + 384), o("RST"))
    act(o("IDB"), o("IDF"))
    act(o("NIB"), o("IDF"), -1.0)
    for s in range(16):
        act(o("LS", 128 * s + s, 128 * s + 128, 16), o("MG", 0, 128, 16), 16.0)
    for k in range(16):
        q = "s" if k % 2 == 0 else "a"
        dma(q, T.FAW[k:128:16, 0:V], T.FAD[:], [("FAW%d" % k, 0, V)], [("FAD", 0, V)], sem="d18" if q == "s" else "d19")
    dma("s", T.KDW[:, 0:V], T.kd[:], [("KDW", 0, V)], [])
    acc["FAW"] = [(0, V, True, "d18", 128, "dma"), (0, V, True, "d19", 128, "dma")]
    ts(o("WTF"), o("WTI"), 1.0 / 16, OP.mult)
    act(o("LW"), o("LS"), o("WTF"))
    act(o("IHB"), o("IDF"), 0.5)
    act(o("NIF"), o("IDF"), -1.0)
    ms(o("XW", V, RT), 0.0)
    ms(o("PR0"), 0.0)
    ms(o("PR1"), 0.0)
    for k in range(4):
        ms(o("PR0", 32 * k, 32 * k + 16), 2.0 ** -12)
        ms(o("PR1", 32 * k + 16, 32 * k + 32), 2.0 ** -12)
    iota(o("PMI"), [[1, 1]], 0, 1)
    iota(o("L16"), [[16, 12]], 0, 0)
    iota(o("LD"), [[-16, 12]], 176, 0)
    iota(o("TIN"), [[1, 16]], 0, 0)
    asel(o("REV"), o("ONE"), [[-16, 8], [1, 16]], OP.is_equal, -15, 1)
    iota(o("CJ"), [[0, 12], [-1, 16]], 15, 0)
    asel(o("P00"), o("PR0"), [[-1, 128]], OP.is_equal, 0, 1)
    asel(o("P11"), o("PR1"), [[-1, 128]], OP.is_equal, 0, 1)
    asel(o("P01"), o("PR1"), [[-1, 128]], OP.is_equal, 16, 1)
    asel(o("P10"), o("PR0"), [[-1, 128]], OP.is_equal, -16, 1)
    dma("gq", T.XW[:, 0:V], T.xs[:], [("XW", 0, V)], [])
    iota(o("IOT"), [[1, V]], 0, 0)
    send(0)
    tt(o("D64"), o("IDF", 0, 64), o("IDF", 64, 128), OP.add)
    tt(o("D32"), o("D64", 0, 32), o("D64", 32, 64), OP.add)
    tt(o("MW", 0, 16), o("D32", 0, 16), o("D32", 16, 32), OP.add)
    for a0, n in ((16, 16), (32, 32), (64, 64), (128, 128), (256, 128)):
        cp(o("MW", a0, a0 + n), o("MW", 0, n))
    do("v", lambda: g.vector.tensor_copy(T.PAF[0:8, :], T.PAI[0:8, :]), [("PAF", 0, 384)], [("PAI", 0, 384)])
    do("p", lambda: g.tensor.matmul(T.PC[:, 0:384], T.B8[0:8, :], T.PAF[0:8, :], True, True), [("PC", 0, 384)], [("B8", 0, 128), ("PAF", 0, 384)])
    ts(o("PMJ"), o("PMI"), 15, OP.bitwise_and)
    ms(o("MK"), 1.0)
    cp(o("PMF"), o("PMJ"))
    tt(o("G"), o("PC", 0, 384), o("MW"), OP.mult)
    ts(o("PM2"), o("PMF"), -1.0, OP.mult, 15.0, OP.add)
    ts(o("PN"), o("L16"), o("PMF"), OP.add)
    ts(o("LN"), o("LD"), o("PMF"), OP.add)
    ts(o("MK", 0, 16), o("TIN"), o("PM2"), OP.is_gt)
    scan(o("SD"), o("RST"), o("G"), OP.mult, OP.add)
    for c in range(12):
        cp((T.CC[:, c:13 + c:12], [("CC", c, c + 1), ("CC", c + 12, c + 13)]), o("SD", 191 - 16 * c, 384, 192))
    do("v", lambda: g.vector.tensor_copy(T.U0[:], T.CC[:, 0:24]), [("U0", 0, 24)], [("CC", 0, 24)])

    fill = []

    def step(n=1):
        for _ in range(min(n, len(fill))):
            fill.pop(0)()

    def twelfths(lst, ofs):
        ts(o("N12", 0, 3), o("PN", 0, 3), 1.0 / 12, OP.mult, -11.0 / 24, OP.add)
        ts(o("M12"), o("N12", 0, 3), -12.0, OP.mult, float(ofs), OP.add)
        tt(o("R12"), o("PN", 0, 3), o("M12"), OP.add)
        cp(o(lst, 0, 3), o("R12"))
    fill += [
        lambda: ts(o("S1"), o("PMF"), 1.0, OP.add),
        lambda: ts(o("S2"), o("PMF"), -8.0, OP.mult, 192.0, OP.add),
        lambda: tt(o("S3"), o("S1"), o("S2"), OP.mult),
        lambda: ts(o("EL", 0, 1), o("S3"), -1.0, OP.add, 1247.0, OP.min),
        lambda: ts(o("KTI"), o("LN"), 1.0 / 3, OP.mult, -1.0 / 3, OP.add),
        lambda: ts(o("XD"), o("LN"), float(DO), OP.add),
        lambda: ts(o("KTF"), o("KTI"), -3.0, OP.mult),
        lambda: ts(o("BS", 12, 24), o("PN"), float(UO), OP.add),
        lambda: tt(o("KT3"), o("LN"), o("KTF"), OP.add),
        lambda: ts(o("SL"), o("LN", 0, 3), 977.0, OP.mult),
        lambda: ts(o("E1C"), o("KT3"), 64.0, OP.mult, float(RT), OP.add),
        lambda: twelfths("LQ", 12),
        lambda: twelfths("LE", 24)]
    for c in range(1, 12):
        act(o("MK", 8 * c * (25 - c), 8 * c * (25 - c) + 16), o("MK", 0, 16))
    for k in range(4):
        act(o("D4", 12 * k, 12 * k + 12), o("LN"), 1.0, float(V + 192 * (k % 2)))

    def r3(n, ap, lo, hi):
        return ap, [(n, lo, hi)]

    def qq(k, side=None):
        if side is None:
            return T.QQ[:, k, :, :], [("QQ", 24 * k, 24 * k + 24)]
        return T.QQ[:, k, side, :], [("QQ", 24 * k + 12 * side, 24 * k + 12 * side + 12)]

    for rnd in range(RO):
        last = rnd == RO - 1
        for k in range(3):
            tt(o("G"), ind("FAW", 0, V, "U%d" % k, 0, 24), o("MW"), OP.mult)
            step()
            scan(o("SB", 384 * k, 384 * k + 384), o("RST"), o("G"), OP.mult, OP.add)
            y = o("SB", 384 * k + 15, 384 * k + 384, 16)
            ya = o("SB", 384 * k + 15, 384 * k + 192, 16)
            step()
            if k < 2:
                cp(o("U%d" % (k + 1)), y)
            step()
            for row in ((k, k + 3) if k < 2 else (k,)):
                act(r3("Y", T.Y[:, row, 0:24], 36 * row, 36 * row + 24), y)
                act(r3("Y", T.Y[:, row, 24:36], 36 * row + 24, 36 * row + 36), ya)
        cp(o("CC", 24, 96), o("SB", 15, 1152, 16))
        tt(o("DL"), o("CC", 0, 72), o("CC", 24, 96), OP.subtract)
        for r in range(3):
            tt(r3("E%d" % r, T["E%d" % r][:], 0, 3), r3("Y", T.Y[:, 0:3, 0:24], 0, 108), r3("Y", T.Y[:, r:r + 3, 12:36], 36 * r, 36 * r + 108), OP.is_equal)
        tt(r3("E0", T.E0[:], 0, 3), r3("E0", T.E0[:], 0, 3), r3("E1", T.E1[:], 0, 3), OP.max)
        step(2)
        tt(o("H"), r3("E0", T.E0[:], 0, 3), r3("E2", T.E2[:], 0, 3), OP.max)
        step()
        tt(o("H", 24, 48), o("H", 0, 24), o("H", 24, 48), OP.max)
        step()
        tt(o("H", 48, 72), o("H", 24, 48), o("H", 48, 72), OP.max)
        step(len(fill))
        tt(o("PRD"), o("DL"), o("H"), OP.mult)
        tt(o("PF", 0, 12), o("H", 0, 12), o("DL", 24, 36), OP.mult)
        tt(o("T1"), o("PRD", 0, 24), o("PRD", 24, 48), OP.add)
        tt(o("T2"), o("PRD", 48, 72), o("CC", 72, 96), OP.add)
        tt(o("PF", 12, 24), o("H", 24, 36), o("DL", 48, 60), OP.mult)
        do("v", lambda: g.vector.tensor_tensor(T.QQ[:, 0, :, :], o("T1")[0], o("T2")[0], OP.add), [("QQ", 0, 24)], o("T1")[1] + o("T2")[1])
        tt(o("F1"), o("PF", 0, 12), o("PF", 12, 24), OP.add)
        do("v", lambda: g.vector.tensor_copy(T.UAB[:], T.QQ[:, 0, :, :]), [("UAB", 0, 24)], [("QQ", 0, 24)])
        tt(o("NE"), qq(0, 0), qq(0, 1), OP.not_equal)
        cp(o("KL", 0, 192), ind("KDW", 0, V, "UAB", 0, 12))
        act(o("XAB"), ind("XW", 0, V, "UAB", 0, 24))
        mm(o("PD", 0, 12), o("REV"), qq(0, 0), True, True)
        mm(o("PXP", 0, 384), o("IDB"), o("XAB"), True, True)
        for hf in range(2):
            l0, l1 = PARTS[hf]
            act(o("XA", 16 * l0, 16 * l1), ind("XW", 0, V, "KL", l0, l1))
        cp(o("KL", 192, 384), ind("KDW", 0, V, "UAB", 12, 24))
        for hf in range(2):
            l0, l1 = PARTS[hf]
            act(o("XB", 16 * l0, 16 * l1), ind("XW", 0, V, "KL", 192 + l0, 192 + l1))
        cp(r3("KF", T.KF[:], 0, 12), o("KL"))
        for gp in range(2):
            for cq in range(2):
                mm((T.PMX[:, :, 16 * gp:16 * gp + 16], [("PMX", 0, 12)]), o("P%d%d" % (gp, cq)), (T.KF[:, :, cq, :], [("KF", 0, 12)]), cq == 0, cq == 1)
        tt(o("FW"), o("F1"), o("CC", 72, 84), OP.add)
        tt(o("ME2", 0, 12), o("NE"), o("H", 48, 60), OP.mult)
        cp(o("UR"), o("PD", 0, 12))
        cp(o("FR"), ind("FAW", 0, V, "UR", 0, 12))

        def equal_f(c):
            e0 = 8 * c * (25 - c)
            ts(o("EQ", e0, e0 + 192 - 16 * c), o("FR", 16 * c, 192), o("FW", c, c + 1), OP.is_equal)
        for c in range(NEQ):
            equal_f(c)
        for sd in range(2):
            xn, mn, gn, pk = ("XA", "XB")[sd], ("MA", "MB")[sd], ("GA1", "GB1")[sd], ("PKA", "PKB")[sd]
            for hf in range(2):
                l0, l1 = PARTS[hf]
                for j in range(0 if sd and hf in PE_HALVES else 16):
                    tt(r3("%s_%d" % (mn, j), T[mn][:, l0:l1, j], l0, l1), o(xn, 16 * l0 + j, 16 * l1, 16), o("PXP", 192 * (1 - sd) + l0, 192 * (1 - sd) + l1), OP.max)
                mm(o(pk, l0, l1), o("IDB"), o("CJ", l0, l1), True, False)
                for s in range(16):
                    mm(o(pk, l0, l1), o("LS", 128 * s, 128 * s + 128), (T[mn][:, l0 + s:l1:16, :], [("%s_%d" % (mn, j), l0, l1) for j in range(16)]), False, s == 15)
                scan(o(gn, 16 * l0, 16 * l1), o("RSB", 16 * l0, 16 * l1), o(xn, 16 * l0, 16 * l1), OP.mult, OP.max)
            for hf in (() if sd else PE_HALVES):
                l0, l1 = PARTS[hf]
                for j4 in range(4):
                    pb = ("PC", "PH", "PD")[j4 % 3]
                    for j in range(4):
                        po = o(pb, j, 4 * (l1 - l0), 4)
                        mm(po, o("IDB"), o("XB", 16 * l0 + 4 * j4 + j, 16 * l1, 16), True, False)
                        mm(po, o("NIB"), o("XAB", l0, l1), False, True)
                    do("a", lambda: g.scalar.activation(T.MB[:, l0:l1, 4 * j4:4 * j4 + 4], T[pb][:, 0:4 * (l1 - l0)], AF.Relu),
                       [("MB_%d" % (4 * j4 + j), l0, l1) for j in range(4)], [(pb, 0, 512)])
            if sd == 0:
                do("v", lambda: g.vector.transpose(T.PS[:], T.PMX[:]), [("PS", 0, 12)], [("PMX", 0, 12)])
                fill += [lambda c=c: equal_f(c) for c in range(NEQ, 12)]
                step(len(fill) - 5)
            else:
                scan(o("EQS"), o("EQ"), o("MK"), OP.max, OP.mult)
                if not last:
                    tt(o("G"), o("MW"), r3("PS", T.PS[:], 0, 12), OP.mult)
                    scan(o("SD"), o("RST"), o("G"), OP.mult, OP.add)
                fill += [lambda: ts(o("CM"), ind("EQS", 0, 1248, "EL", 0, 1), -1.0, OP.mult, 1.0, OP.add),
                         lambda: tt(o("CU"), o("CM", 0, 12), o("UN"), OP.mult)]
            scan(o("RUN"), o("RST", 0, 192), o(pk, 0, 192), OP.mult, OP.max)
            step()
            tt(o("TT"), o("RUN"), o(pk, 0, 192), OP.subtract)
            step()
            tt(o("DD"), r3("PS", T.PS[:, 6 * sd:6 * sd + 6, :], 6 * sd, 6 * sd + 6), o("TT"), OP.subtract)
            step()
            scan(o("LSC"), o("TT"), o("DD"), OP.min, OP.max)
            step()
            le = o("LSC", 15, 192, 16)
            ts(o("UL3", 12 * sd, 12 * sd + 12), le, 4096.0, OP.mult)
            step()
            cp(o("K2", 192 * sd, 192 * sd + 192), ind("KDW", 0, V, "UL3", 12 * sd, 12 * sd + 12))
            act(qq(1, sd), le, 4096.0)
            if sd == 0:
                act(o("ME2", 12, 24), o("ME2", 0, 12))
                act(o("UN"), o("ME2", 0, 12), -1.0, 1.0)
                act(o("THR", 0, 12), o("ME2", 0, 12), -4096.0, 4096.0 + 143.0)
                act(o("THR", 12, 24), o("ME2", 0, 12), -4096.0, 4096.0 + 143.0)
                act(o("B2", 0, 12), o("E1C"), 1.0, float(192 * rnd))
                ts(o("UL3", 24, 36), le, 4096.0, OP.mult)
            k2 = 192 * sd
            act(o(("YA", "YB")[sd], 0, 1536), ind("XW", 0, V, "K2", k2, k2 + 96))
            if sd == 0:
                act(o("YA", 1536, 3072), ind("XW", 0, V, "K2", 96, 192))
            else:
                act(o("YB", 1536, 16 * VL), ind("XW", 0, V, "K2", 288, 192 + VL))
                if VL < 192:
                    cp(o("YB", 16 * VL, 3072), ind("XW", 0, V, "K2", 192 + VL, 384))
                if not last:
                    act(qq(2), o("SD", 15, 384, 16), 4096.0)
                    act(o("LR"), ind("IOT", 0, V, "UL3", 0, 24))
                act(o("FV"), ind("FAW", 0, V, "UL3", 12, 36))
        for s in range(16):
            kw = o("LW", 128 * s, 128 * s + 128)
            mm(o("PH", 0, 12), kw, o("GA1", 16 * s + 15, 3072, 256), s == 0, False)
            if not last:
                mm(r3("PS", T.PS[:, 0, 0:3], 0, 12), kw, o("GB1", 16 * s + 15, 768, 256), s == 0, False)
        lf = qq(1)
        ts(o("ZF"), lf, float(Z), OP.is_equal)
        tt(o("ZD"), qq(0), lf, OP.subtract)
        tt(o("NZ"), o("ZF", 0, 12), o("ZF", 12, 24), OP.max)
        tt(o("ZP"), o("ZD"), o("ZF"), OP.mult)
        ts(o("NZ2"), o("NZ"), -1.0, OP.mult, 1.0, OP.add)
        tt(qq(3), lf, o("ZP"), OP.add)
        if last:
            cp(qq(2), qq(1))
        for sd in range(2):
            xn, gn = ("YA", "YB")[sd], ("GA2", "GB2")[sd]
            for hf in range(2):
                l0, l1 = 1536 * hf, 1536 * hf + 1536
                scan(o(gn, l0, l1), o("RSB", l0, l1), o(xn, l0, l1), OP.mult, OP.max)
            if sd == 0:
                mm(o("PC", 0, 192), o("IHB"), o("GA1", 15, 3072, 16), True, False)
                mm(o("PC", 0, 192), o("IHB"), o("GA2", 15, 3072, 16), False, True)
                act(o("XW", UO, UO + 192), o("PC", 0, 192))
            for s in range(16):
                kw = o("LW", 128 * s, 128 * s + 128)
                if sd == 0:
                    mm(o("PH", 0, 12), kw, o("GA2", 16 * s + 15, 3072, 256), False, s == 15)
        mm(o("PD", 0, 192), o("IDB"), o("GA1", 15, 3072, 16), True, False)
        mm(o("PD", 0, 192), o("NIB"), o("GB1", 15, 3072, 16), False, False)
        mm(o("PD", 0, 192), o("IDB"), o("GA2", 15, 3072, 16), False, False)
        mm(o("PD", 0, 192), o("NIB"), o("GB2", 15, 3072, 16), False, True)
        if not last:
            for s in range(16):
                mm(r3("PS", T.PS[:, 0, 0:3], 0, 12), o("LW", 128 * s, 128 * s + 128), o("GB2", 16 * s + 15, 768, 256), False, s == 15)
        ts(o("CMP", 0, 192), o("PD", 0, 192), 0.0, OP.is_gt)
        ts(o("CMP", 192, 384), o("PD", 0, 192), 0.0, OP.is_lt)
        for s in range(16):
            mm(o("PC", 0, 24), o("LS", 128 * s, 128 * s + 128), o("CMP", s, 384, 16), s == 0, s == 15)
        do("v", lambda: g.vector.tensor_tensor(T.QD[:], T.QQ[:, :, 1, :], T.QQ[:, :, 0, :], OP.subtract), [("QD", 0, 48)], [("QQ", 0, 96)])
        do("v", lambda: g.vector.tensor_tensor(T.E4[:], T.QQ[:, 0:2, :, :], T.D4[:], OP.subtract), [("E4", 0, 48)], [("QQ", 0, 48), ("D4", 0, 48)])
        tt(o("CN"), o("CM", 0, 12), o("NZ2"), OP.mult)
        cp(o("HI"), o("PH", 0, 12))
        ts(o("HJ"), o("HI"), 63, OP.bitwise_and)
        if not last:
            tt(o("SH"), o("HI", 0, 3), o("SL"), OP.add)
        tt(o("BS", 0, 12), o("B2", 0, 12), o("HJ"), OP.add)
        tt(o("WB", 0, 24), o("PC", 0, 24), o("THR"), OP.is_ge)
        xe = RT + 192 * rnd + 192

        def new_x(xe=xe, last=last):
            return [
                lambda: tt(o("OK1"), o("CM", 0, 12), o("WON"), OP.mult),
                lambda: tt(o("DX"), o("Q", 0, 12), o("XD"), OP.subtract),
                lambda: tt(o("OK2"), o("OK1"), o("CU"), OP.add),
                lambda: tt(o("XS"), ind("XW", 0, xe, "EU", 0, 12), o("XE"), OP.add),
                lambda: tt(o("DX2"), o("DX"), o("OK2"), OP.mult),
                lambda: ts(o("XN"), o("XS"), 0.5, OP.mult, -0.375, OP.add),
                lambda: tt(o("DX"), o("XD"), o("DX2"), OP.add),
                lambda: None if last else cp(scat("KDW", 0, 2176, "DU", 0, 24), o("NK")),
                lambda: cp(o("XU"), o("DX")),
                lambda: cp(scat("XW", 0, RT, "XU", 0, 12), o("XN"))]

        def new_k():
            def half(h0):
                tt(o("NK", 32 * h0, 32 * h0 + 192), r3("KF", T.KF[:, h0:h0 + 6, :, :], h0, h0 + 6), o("MM", 32 * h0, 32 * h0 + 192),
                   OP.subtract if h0 else OP.add)
            return [
                lambda: tt(o("OH"), r3("KF", T.KF[:], 0, 12), o("PKB", 0, 384), OP.is_equal),
                lambda: tt(o("MM", 0, 192), o("OH", 0, 192), o("PKA", 0, 192), OP.mult),
                lambda: tt(o("MM", 192, 384), o("OH", 192, 384), o("PKA", 0, 192), OP.mult),
                lambda: half(0),
                lambda: half(6)]

        if not last:
            mm(o("PKB", 0, 384), o("IDF"), o("LR"), True, True)
            mm(o("PKA", 0, 192), o("IDF"), o("LR", 192, 384), True, False)
            mm(o("PKA", 0, 192), o("NIF"), o("LR", 0, 192), False, True)
        tt(o("WON"), o("WB", 0, 12), o("WB", 12, 24), OP.add)
        tt(o("QP"), ind("WB", 0, 24, "LQ", 0, 3), o("QD"), OP.mult)
        tt(o("WB", 24, 36), o("CN"), o("WON"), OP.mult)
        do("v", lambda: g.vector.tensor_tensor(T.Q[:], T.QQ[:, :, 0, :], T.QP[:], OP.add), [("Q", 0, 48)], [("QQ", 0, 96), ("QP", 0, 48)])
        tt(o("EP"), ind("WB", 0, 36, "LE", 0, 3), o("E4"), OP.mult)
        tt(o("B2"), o("Q", 0, 24), o("BS"), OP.subtract)
        tt(o("DS"), o("D4"), o("EP"), OP.add)
        tt(o("B3"), o("B2"), o("ME2"), OP.mult)
        if not last:
            tt(o("SI"), r3("PS", T.PS[:, 0, 0:3], 0, 12), o("SH"), OP.add)
        cp(o("DU"), o("DS"))
        tt(o("B2"), o("BS"), o("B3"), OP.add)
        if not last:
            ts(o("SJ"), o("SI"), 2047, OP.bitwise_and)
        cp(o("EU"), o("B2"))
        act(o("XE"), ind("XW", 0, xe, "EU", 12, 24))
        if last:
            for p in new_x():
                p()
            dma("gq", T.yx[:], T.XW[:, 0:V], [("yx", 0, V)], [("XW", 0, V)])
            cp(scat("FAW", 0, 2176, "DU", 24, 48), o("FV"))
            dma("s", T.YFA[:], T.FAW[0:128:16, 0:V], [("YFA", 0, 112)], [("FAW", 0, V)])
            tt(o("YFB"), o("YFA"), o("DPF"), OP.subtract)
            dma("s", T.yf[:], T.YFB[:], [("yf", 0, V)], [("YFB", 0, 112)])
            break
        cp(o("CC", 0, 12), o("Q", 36, 48))
        ts(o("SF"), o("SJ"), float(V), OP.is_ge, float(V), OP.mult)
        cp(o("CC", 15, 24), o("Q", 27, 36))
        tt(o("CC", 12, 15), o("SJ"), o("SF"), OP.subtract)
        cp(scat("FAW", 0, 2176, "DU", 24, 48), o("FV"))
        cp(o("U0"), o("CC", 0, 24))
        fill += new_k() + new_x() + [lambda rnd=rnd: send(rnd + 1)]
    for s, n in total.items():
        if waited.get(s, 0) < n:
            g.wait_ge(T.sem[s], n)
